import numpy as np, ml_dtypes
CORES = [10,34,74,98]
N = 4
import mx_ref
BF = ml_dtypes.bfloat16
def gcols(t, e):
    v = np.concatenate([t.reshape(8, 16, -1, 4), np.zeros((8, 16, 1, 4), BF)], axis=2)
    return np.ascontiguousarray(np.stack([v[g][:, e[g]] for g in range(8)])).reshape(128, -1)
def tile(rs):
    return np.stack(rs, axis=2).reshape(128, -1).astype(BF)
def pick(q, e):
    c = np.concatenate([q[0].reshape(128, -1, 4), np.zeros((128, 1, 4), np.uint8)], axis=1); s = np.concatenate([q[1], np.ones((16, 1), np.uint8)], axis=1)
    return (np.ascontiguousarray(c[:, e].reshape(128, -1)), np.ascontiguousarray(s[:, e]))
def join(*qs):
    return (np.concatenate([q[0] for q in qs], axis=1), np.concatenate([q[1] for q in qs], axis=1))
def put(q, e, v):
    c, s = q[0].reshape(128, -1, 4).copy(), q[1].copy(); c[:, e] = v[0].reshape(128, -1, 4); s[:, e] = v[1]
    return (c.reshape(128, -1), s)
def pk(c, s):
    return (np.ascontiguousarray(c), mx_ref.live(s))
def emit(q):
    return q[0], q[1]
def packed(v, rng):
    q = [mx_ref.quantize(np.ascontiguousarray(v[r])) for r in range(N)]
    return np.stack([a for a, b in q]), np.stack([mx_ref.plane(b, rng) for a, b in q])
def values_of_codes():
    e, c = np.zeros((128, 128, 4), np.float32), np.zeros((128, 2, 4), np.uint8)
    e[np.arange(128), np.arange(128), 0] = 1
    c[:127, :, 0] = np.arange(256).reshape(2, 128).T[:127]
    return mx_ref.matmul(mx_ref.quantize(e.reshape(128, 512).astype(BF)), (c.reshape(128, 8), np.full((16, 2), 127, np.uint8))).T.reshape(-1).astype(np.float64)
CODE_VALUE, SCALE_VALUE = values_of_codes(), 2.0 ** (np.arange(256) - 127.0)
def decode(q):
    return (CODE_VALUE[q[0]].reshape(16, 8, -1, 4) * SCALE_VALUE[q[1]][:, None, :, None] + 0.0).reshape(128, -1).astype(np.float32)
def f(rng, *shape):
    return mx_ref.flush((rng.standard_normal(shape, dtype=np.float32) * np.exp2(rng.integers(-2, 3, shape[:-1] + (1,)))).astype(BF))
def wide(rng, *shape, cols=0):
    v = rng.standard_normal(shape, dtype=np.float32) * np.exp2(rng.integers(-12, 13, shape)).astype(np.float32)
    if cols: v *= np.repeat(np.exp2(rng.integers(-cols, cols + 1, shape[:-2] + (1, shape[-1] // 4))) * (rng.random(shape[:-2] + (1, shape[-1] // 4)) > 0.0625), 4, axis=-1).astype(np.float32)
    return mx_ref.flush(v.astype(BF))
C, H, M, R = 448, 5, 32, 2
def keys(p):
    b = p.reshape(8, 16, -1)[:, :H] > 0
    return np.sum(b * (1 << np.arange(H))[:, None], axis=1)
def cells(a, key):
    a = a.reshape(8, 16, C, 4)
    c = np.zeros((8, 16, M, 4), np.float32)
    for g in range(8):
        for k in np.unique(key[g]): c[g, :, k] = np.max(a[g][:, key[g] == k], axis=1)
    return c.reshape(128, 4 * M).astype(BF)
def big(v, k):
    v = v.astype(np.float32) * np.float32(k)
    v[np.abs(v) < np.float32(2.0 ** -16)] = 0
    return v.astype(BF)
def weights(rng, k, still=0):
    w = big(f(rng, 128, 2048), k).reshape(128, 4, 128, 4)
    w[:, :, np.arange(128) % 16 < still] = 0
    w = w.reshape(128, 2048)
    c, p = packed(np.stack([w] * N), rng)
    return {"wc": c, "ws": p}
def numbers_of(rng):
    return {"x": big(f(rng, N, 128, 4 * C), 1), "u": np.array(f(rng, N, 128, 512)), "v": np.array(f(rng, N, 128, 512))}
def aim(d, x, key, size):
    u = d["u"].reshape(N, 128, 128, 4)
    for i in range(H):
        x[:, :, i // 4, :, i % 4] = np.where((key >> i) & 1, size, -size)
        for g in range(8):
            u[:, :, 16 * g + i] = 0
            u[:, 16 * g + i // 4, 16 * g + i, i % 4] = 1
def setup_inputs(rng):
    return {**numbers_of(rng), **weights(rng, 1)}
def setup_inputs_ties(rng):
    d = numbers_of(rng)
    d["u"].reshape(N, 8, 16, 128, 4)[:, :, 8:] = 0
    x = d["x"].reshape(N, 8, 16, C, 4)
    e = rng.permutation(N)
    for r in range(N):
        a = x[r][:, :, :1].copy()
        k = rng.permutation(C) % 4
        if r == e[1]: k[:] = 2
        x[r][:, :, k == 0] = 0
        x[r][:, :8, k == 1] = 0
        x[r][:, :, k == 2] = a
    x[e[0]] = 0
    return {**d, "x": x.reshape(N, 128, 4 * C), **weights(rng, 1)}
def setup_inputs_near(rng):
    d = numbers_of(rng)
    x = rng.integers(4, 8, (N, 8, 16, C, 4)) * rng.choice([-0.25, 0.25], (N, 8, 16, C, 4))
    x[:, :, :8] = 0
    s = rng.choice([-1.0, 1.0], (N, 8, C))
    x[:, :, 8, :, 0] = s
    x[:, :, 9, :, 0] = -s
    o = rng.permutation(N)
    a = int(np.argmax(o == 1))
    x[a, :, 8:10, :, 0] = 0
    x[a, :, 7, :, 0] = -s[a] * 2.0 ** -27
    k = np.where(o % 2 == 0, 1.0, 2.0 ** -30).astype(np.float32).astype(BF)
    u = d["u"].reshape(N, 128, 128, 4)
    for i in range(H):
        c = rng.choice([-1.0, 0.0, 1.0, 1.0], (N, 8, C))
        x[:, :, i // 4, :, i % 4] = c * 2.0 ** -23
        x[a, :, i // 4, :, i % 4] = (s[a] + c[a] * 0.125) * 2.0 ** -27
        for g in range(8):
            u[:, :, 16 * g + i] = 0
            u[:, 16 * g + i // 4, 16 * g + i, i % 4] = k
            u[:, 16 * g + 7:16 * g + 10, 16 * g + i, 0] = k[:, None]
    return {**d, "x": x.astype(np.float32).reshape(N, 128, 4 * C).astype(BF), **weights(rng, 1, 10)}
def setup_inputs_huge(rng):
    d = numbers_of(rng)
    key = np.stack([np.stack([rng.permutation(C) % M for g in range(8)]) for r in range(N)])
    sign = np.stack([rng.permutation(M) % 2 * 2.0 - 1.0 for g in range(8)])
    size = rng.integers(8, 17, (N, 8, 16, C, 4))
    size[..., :2] = 16
    x = size * 2.0 ** 26 * sign[np.arange(8)[:, None], key][:, :, None, :, None]
    aim(d, x, key, 2.0 ** 30)
    d["u"] = big(d["u"], 2.0 ** 25)
    return {**d, "x": x.astype(np.float32).reshape(N, 128, 4 * C).astype(BF), **weights(rng, 2.0 ** -3, 2)}
def setup_inputs_crowd(rng):
    d = numbers_of(rng)
    e = rng.permutation(N)
    half = rng.permutation(8) < 4
    nil = rng.permutation(8) < 2
    p = int(e[3]) * (M // N) + M // N - 2
    gone = rng.choice([r for r in range(1, N) if r != e[3]])
    there = np.array([k for k in range(M) if k // (M // N) != gone and k not in (p, p + 1)])
    j = rng.permutation(C)
    key, low = np.zeros((N, 8, C), int), np.zeros((N, 8, C), bool)
    for g in range(8):
        c = rng.permutation(there)
        if nil[g]: c = np.concatenate([[0], c[c != 0]])
        for r in range(N):
            k = np.concatenate([c[:1], rng.choice(c[2:], C - 1)])
            if r == e[1] or r == e[0] and half[g]: k[:] = c[0]
            if r == e[2]: k = np.resize(c, C)
            if r == e[3]: key[r, g, j] = np.concatenate([[p, p + 1, p + 1], rng.permutation(k[:-3])])
            else: key[r, g] = rng.permutation(k)
        low[:, g] = (key[:, g] == c[0]) | (key[:, g] == c[1])
    x = d["x"].astype(np.float32).reshape(N, 8, 16, C, 4)
    x = np.where(low[:, :, None, :, None], -1 - np.abs(x), x)
    a = x[e[1]]
    a[:, 2:, 0, 1] = 0
    a[:, 2:, -1, 2] = 0
    b = x[e[3]]
    b[:, 8:, j[0]] = (1 + rng.random((8, 8, 4))) * np.exp2(rng.integers(-1, 4, (8, 8, 4)))
    b[:, 15, j[0], 3] = -127 * 2.0 ** 10
    b[:, 8:, j[1]] = 1 + rng.random((8, 8, 4))
    b[:, 15, j[1], 3] = -2.0 ** 22
    b[:, 8:, j[2]] = -1 - rng.random((8, 8, 4))
    aim(d, x, key, 1.0)
    a[nil, :, -1] = 0
    return {**d, "x": x.astype(np.float32).reshape(N, 128, 4 * C).astype(BF), **weights(rng, 1, 2)}
def setup_inputs_spread(rng):
    d = setup_inputs(rng)
    d["x"] = big(wide(rng, N, 128, 4 * C, cols=6), 1)
    return d
def check_inputs(d):
    b = []
    for k in ("x", "u", "v"):
        a = np.abs(d[k].astype(np.float32))
        if not (np.isfinite(a).all() and ((a == 0) | (a >= 2.0 ** -30) & (a <= 2.0 ** 30)).all()): b.append("a value of " + k)
    if (d["wc"] != d["wc"][:1]).any(): b.append("wc differs between ranks")
    s = [mx_ref.live(p) for p in d["ws"]]
    if any((p != s[0]).any() for p in s): b.append("ws differs between ranks")
    try:
        a = np.abs(decode(pk(d["wc"][0], d["ws"][0])))
        m = np.max(a.reshape(16, 8, 512, 4), axis=(1, 3))
        good = bool(np.isfinite(a).all() and ((m == 0) | (m >= 2.0 ** -30) & (m <= 2.0 ** 30)).all())
    except Exception:
        good = False
    if not good: b.append("a value of W")
    return b
def reference(x, u, v, wc, ws):
    w = pk(wc[0], ws[0])
    qu = [mx_ref.quantize(u[r]) for r in range(N)]
    now = [x[r] for r in range(N)]
    kl = np.zeros((N, 8 * R, C), np.float32)
    for t in range(R):
        held, key, made = [], [], []
        for r in range(N):
            q = mx_ref.quantize(now[r])
            key.append(keys(mx_ref.matmul(qu[r], q)))
            held.append(decode(q))
            made.append(mx_ref.quantize(cells(held[r], key[r])))
            kl[r, 8 * t:8 * t + 8] = key[r]
        merged = np.max(decode(join(*made)).reshape(128, N, 4 * M), axis=1)
        z = mx_ref.quantize(np.ascontiguousarray(merged.astype(BF)))
        g = tile([np.maximum(mx_ref.matmul(pick(w, np.arange(128 * b, 128 * b + 128)), z), np.float32(0.0)) * np.float32(0.015625) for b in range(4)])
        back = decode(mx_ref.quantize(g)).astype(BF)
        for r in range(N):
            now[r] = ((held[r] + gcols(back, key[r]).astype(np.float32)) * np.float32(0.5)).astype(BF)
    y = np.zeros((N, 128, C), np.float32)
    oc, osc = np.zeros((N, 128, 4 * C), np.uint8), np.zeros((N, 16, C), np.uint8)
    for r in range(N):
        q = mx_ref.quantize(now[r])
        y[r] = mx_ref.matmul(mx_ref.quantize(v[r]), q)
        oc[r], osc[r] = emit(q)
    return {"y": y, "kl": kl, "oc": oc, "osc": osc}

@@ -1,0 +1,472 @@
+from concourse.bass import DstId, RemoteDMATransfer
+from concourse.mybir import dt, AluOpType, AxisListType, ActivationFunctionType
+
+ALU = AluOpType
+AF = ActivationFunctionType
+C, HC, M, ROUNDS = 448, 224, 32, 2
+CUT = 320
+RUNS = ((0, CUT), (CUT, C))
+F16 = "float16"
+OW = 496
+TBW = 464
+BF, F32, I32, U16, CODE, PLANE = "bfloat16", "float32", "int32", "uint16", "float8_e4m3fn_x4", "uint8"
+
+WIDTHS = {
+    BF: dict(st0=4 * C, st1=4 * C, st2=4 * C, us=512, vs=512, ones=516, f1=516, fh=516, bt=4 * C, stt=1024,
+             stk=512, bs=128, mw=C, mr=C, tb=2 * TBW, jv=512, sw=704, dh=4 * C, gs=4 * C, oo=4 * OW + 16,
+             mm0=OW, mm1=OW, nb=32, at=512, ya=256, y2=256, zz=512, gt=512, gw=128,
+             tm=2 * CUT + 4 * (C - CUT)),
+    F32: dict(tf=32, sig=32, mwf=128, rf=32, wk0=32, wks=1, wk=1, dmf=16, m16a=16, m16b=16, cst=6, th=4,
+              dc=6, ndm=1, corr=1, dum=2, ct=64, ctt=64, ci=40, bx=32, bxs=2, s4=4, se=4, eb=2, ed=2,
+              kf0=C, kf1=C, yf=C),
+    I32: dict(pi=1, ti=5, mwi=128, mwj=128, dmi=16, dmj=16),
+    F16: dict(ta=2 * C, zs=2 * C, zt=2 * C, rb=1024, wt=32, wr=C, kr=C),
+    U16: dict(wo=32, lo=28, so=4, ko=28),
+    CODE: dict(xq0=C, xq1=C, xq2=C, uq=128, vq=128, wq=512, ehq=512, e1q=512, bq=C, stq=256, skq=128,
+               lq0=224, lq1=224, zq=128, gq=128),
+    PLANE: dict(xp0=C, xp1=C, xp2=C, up=128, vp=128, wp=512, ehp=512, e1p=512, bp=C, stp=256, skp=128,
+                lp0=224, lp1=224, zp=128, gp=128),
+}
+SCRATCH = {}
+for _dtype, _bufs in WIDTHS.items():
+    for _name, _w in _bufs.items():
+        SCRATCH[_name] = ("sbuf", [128, _w], _dtype)
+for _k in range(8):
+    SCRATCH["pb%d" % _k] = ("psum", [128, 512], F32)
+NDMA = 20
+SEMAPHORES = ["qv", "qa", "qt", "qg", "sent", "arr0", "arr1"] + ["d%d" % _k for _k in range(NDMA)]
+
+
+def rank_program(g, core, T, topo):
+    rank = T.rank_of(core)
+    if rank is None:
+        return
+    cores = [int(c) for c in T.cores]
+    n_ranks = len(cores)
+    ops = []
+    eng = {"v": g.vector, "a": g.scalar, "t": g.tensor, "g": g, "s": g.sync}
+
+    def v(name, a=0, b=None, s=1):
+        if b is None:
+            b = SCRATCH[name][1][1]
+        ap = T[name][:, a:b] if s == 1 else T[name][:, a:b:s]
+        cols = frozenset([0]) if name.startswith("pb") else frozenset(range(a, b, s))
+        return (ap, [(name, cols)])
+
+    def ind(win, off):
+        return (win[0].indirect(off[0]), win[1] + off[1])
+
+    def ap(x):
+        return x[0] if isinstance(x, tuple) else x
+
+    def foot(xs):
+        return [f for x in xs if isinstance(x, tuple) for f in x[1]]
+
+    def add(q, kind, fn, reads, writes):
+        ops.append(dict(q=q, kind=kind, fn=fn, r=foot(reads), w=foot(writes)))
+
+    def ts(out, in0, s1, s2, op0, op1=None):
+        if op1 is None:
+            add("v", "c", lambda: g.vector.tensor_scalar(ap(out), ap(in0), ap(s1), None, op0), [in0, s1], [out])
+        else:
+            add("v", "c", lambda: g.vector.tensor_scalar(ap(out), ap(in0), ap(s1), ap(s2), op0, op1),
+                [in0, s1, s2], [out])
+
+    def tt(out, in0, in1, op):
+        add("v", "c", lambda: g.vector.tensor_tensor(ap(out), ap(in0), ap(in1), op), [in0, in1], [out])
+
+    def cp(out, in_):
+        add("v", "c", lambda: g.vector.tensor_copy(ap(out), ap(in_)), [in_], [out])
+
+    def scatter(win, off, in_):
+        add("v", "c", lambda: g.vector.tensor_copy(win[0].indirect(off[0]), ap(in_)), [in_, off], [win])
+
+    def mset(out, val):
+        add("v", "c", lambda: g.vector.memset(ap(out), val), [], [out])
+
+    def scan(out, d0, d1, init, op0, op1):
+        add("v", "c", lambda: g.vector.tensor_tensor_scan(ap(out), ap(d0), ap(d1), ap(init), op0, op1),
+            [d0, d1, init], [out])
+
+    def tr(out, in_):
+        add("v", "c", lambda: g.vector.transpose(ap(out), ap(in_)), [in_], [out])
+
+    def quant(q, p, a, b, tile):
+        add("v", "c", lambda: g.vector.quantize_mx(T[q][:, a:b], T[p][:, a:b], ap(tile)), [tile],
+            [v(q, a, b), v(p, a, b)])
+
+    def act(out, in_, func, bias=None, scale=None, accum=None):
+        kw = {}
+        if bias is not None:
+            kw["bias"] = ap(bias)
+        if scale is not None:
+            kw["scale"] = ap(scale)
+        if accum is not None:
+            kw["accum_out"] = ap(accum)
+        add("a", "c", lambda: g.scalar.activation(ap(out), ap(in_), func, **kw), [in_, bias, scale],
+            [out, accum])
+
+    def mm(bank, lq, lp, la, rq, rp, a, b):
+        sides = [v(lq, la, la + 128), v(lp, la, la + 128), v(rq, a, b), v(rp, a, b)]
+        out = v("pb%d" % bank, 0, b - a)
+        add("t", "c", lambda: g.tensor.matmul_mx(out[0], sides[0][0], sides[1][0], sides[2][0], sides[3][0],
+                                                 True, True), sides, [out])
+
+    def pb(bank, a, b):
+        return v("pb%d" % bank, a, b)
+
+    def iota(out, pattern, base, cm, whole=False):
+        if whole:
+            add("g", "c", lambda: g.iota(ap(out), pattern, base, cm), [], [out])
+        else:
+            add("g", "c", lambda: g.iota(ap(out), pattern, base, cm, allow_small_or_imprecise_dtypes=True),
+                [], [out])
+
+    def zeros(out):
+        iota(out, [[0, len(out[1][0][1])]], 0, 0)
+
+    def sel(out, in_, pattern, op, fill, base, cm):
+        add("g", "c", lambda: g.affine_select(ap(out), ap(in_), pattern, op, fill, base, cm), [in_], [out])
+
+    def dma(q, out, in_, after=()):
+        add(q, "d", lambda: eng[q].dma_start(ap(out), ap(in_)), [in_] + list(after), [out])
+
+    def as_bytes(x):
+        return (x[0].bitcast(dt.uint8), x[1])
+
+    dma("s", v("st0", 0, 4 * CUT), T.x[:, 0:4 * CUT])
+    dma("s", v("us"), T.u[:, :])
+    dma("s", v("st0", 4 * CUT, 4 * C), T.x[:, 4 * CUT:4 * C])
+    dma("s", as_bytes(v("wq")), T.wc[:, :], after=[v("st0")])
+    dma("s", v("wp"), T.ws[:, :])
+    dma("s", v("vs"), T.v[:, :])
+
+    iota(v("pi"), [[0, 1]], 0, 1, True)
+    iota(v("mwi"), [[-16, 8], [0, 16]], 128, 1, True)
+    mset(v("ones"), 1.0)
+    mset(v("tf"), 0.0)
+    iota(v("dmi"), [[1, 16]], 128, -1, True)
+    iota(v("rf"), [[1, 32]], 0, 0)
+    sel(v("f1"), v("ones"), [[1, 516]], ALU.is_equal, 0.0, -3, -4)
+    iota(v("cst", 0, 4), [[-1, 2], [-16, 2]], 1, 0)
+    iota(v("cst", 4, 6), [[16, 2]], C + 16, 0)
+    zeros(v("tb", 0, 2 * TBW, TBW))
+    zeros(v("ct"))
+    zeros(v("ci", 0, 1))
+    iota(v("dum"), [[128, 2]], 513 + C, 1)
+    sel(v("mr"), v("ones", 0, C), [[0, 14], [1, 32]], ALU.is_gt, 0.0, 0, 0)
+    iota(v("jv"), [[1, 32], [32, 16]], -HC, 0)
+
+    for k in range(2):
+        act(v("bt", 512 * k, 512 * k + 512), v("ones", 0, 512), AF.Copy, scale=0.0)
+    for i in range(5):
+        ts(v("ti", i, i + 1), v("pi"), i, 1, ALU.logical_shift_right, ALU.bitwise_and)
+    ts(v("mwj"), v("mwi"), 4, None, ALU.logical_shift_right)
+    ts(v("tf", 0, 5), v("ti"), 2.0, -1.0, ALU.mult, ALU.add)
+    ts(v("tf", 16, 21), v("ti"), 2.0, -1.0, ALU.mult, ALU.add)
+    ts(v("mwf"), v("mwj"), 8.0, None, ALU.is_equal)
+    tr(v("sig"), v("tf"))
+    mset(v("bt", 1024, 4 * C), 0.0)
+    for t in range(4):
+        act(v("bs", t, 128, 4), v("sig"), AF.Copy)
+    ts(v("dmj"), v("dmi"), 15, None, ALU.bitwise_and)
+    tt(v("wk0"), v("sig"), v("rf"), ALU.mult)
+    cp(v("dmf"), v("dmj"))
+    add("v", "c", lambda: g.vector.tensor_reduce(T.wks[:, 0:1], T.wk0[:, :], AxisListType.X, ALU.add),
+        [v("wk0")], [v("wks")])
+    for h in range(2):
+        for a in range(4):
+            dst, col = v("stt", 512 * h + 128 * a, 512 * h + 128 * a + 128), 16 * (2 * a + h)
+            if a < 2:
+                act(dst, v("bs"), AF.Copy, scale=v("mwf", col, col + 1))
+            else:
+                ts(dst, v("bs"), v("mwf", col, col + 1), None, ALU.mult)
+    quant("stq", "stp", 0, 256, v("stt"))
+    act(v("wk"), v("wks"), AF.Copy, scale=1.0 / 32)
+    act(v("fh"), v("f1"), AF.Copy, scale=0.5)
+    for t in range(4):
+        act(v("stk", t, 512, 4), v("mwf"), AF.Copy, scale=v("wk"))
+
+    def unit(q, p, src, b):
+        quant(q, p, 128 * b, 128 * b + 128, v(src, 3 - b, 515 - b))
+
+    def first_products(r):
+        def go(half):
+            a, b = RUNS[half]
+            quant("xq%d" % r, "xp%d" % r, a, b, v("st%d" % r, 4 * a, 4 * b))
+            if r == 0 and half == 0:
+                quant("uq", "up", 0, 128, v("us"))
+            if r < ROUNDS:
+                mm(4 + half, "uq", "up", 0, "xq%d" % r, "xp%d" % r, a, b)
+            else:
+                mm(4 + half, "vq", "vp", 0, "xq%d" % r, "xp%d" % r, a, b)
+                dma("s", T.oc[:, 4 * a:4 * b], as_bytes(v("xq%d" % r, a, b)))
+        return go
+
+    go = first_products(0)
+    go(0)
+    ts(v("m16a"), v("dmf"), 0.0, -4096.0, ALU.is_equal, ALU.mult)
+    ts(v("m16b"), v("dmf"), 1.0, 512.0, ALU.is_equal, ALU.mult)
+    quant("skq", "skp", 0, 128, v("stk"))
+    tt(v("mw", 0, 16), v("m16a"), v("m16b"), ALU.add)
+    go(1)
+    w = 16
+    while w < C:
+        n = min(w, C - w)
+        sel(v("mw", w, w + n), v("mw", 0, n), [[0, n]], ALU.is_ge, 0.0, 0, 0)
+        w += n
+    zeros(v("mm0"))
+    zeros(v("oo", 0, 1))
+    for b in range(4):
+        zeros(v("oo", OW * b + C + 1, OW * (b + 1) + 1))
+    zeros(v("at", 128, 512))
+
+    others = [k for k in range(n_ranks) if k != rank]
+    mask = topo.mask(core, cores[others[0]])
+    for k in others[1:]:
+        mask &= topo.mask(core, cores[k])
+    n_eng = bin(mask).count("1")
+
+    for r in range(ROUNDS):
+        xq, xp, lq, lp, mmr, kf = ["%s%d" % (s, r) for s in ("xq", "xp", "lq", "lp", "mm", "kf")]
+
+        def held(b):
+            mm(b, "ehq", "ehp", 128 * b, xq, xp, 0, C)
+
+        bank = {(0, 0): 6, (1, 0): 7, (0, 1): 4, (1, 1): 5}
+        for k, (a, b) in enumerate(RUNS):
+            act(v("bt", 4 * a, 4 * b, 4), pb(4 + k, 0, b - a), AF.Sign, bias=-1e-36)
+            quant("bq", "bp", a, b, v("bt", 4 * a, 4 * b))
+        if r:
+            held(0)
+            cp(v("dh", 0, C), pb(0, 0, C))
+        else:
+            act(v("ndm"), v("dmf", 15, 16), AF.Copy, scale=-1.0)
+            act(v("th"), v("cst", 0, 4), AF.Identity, bias=v("dmf", 15, 16))
+            act(v("dc", 0, 2), v("cst", 4, 6), AF.Identity, bias=v("ndm"))
+        for k, (a, b) in enumerate(RUNS):
+            for h in range(2):
+                mm(bank[h, k], "stq", "stp", 128 * h, "bq", "bp", a, b)
+        if r == 0:
+            for b in range(4):
+                unit("ehq", "ehp", "fh", b)
+            held(0)
+
+        def match(h, k):
+            a, b = RUNS[k]
+            act(v("tb", TBW * h + 1 + a, TBW * h + 1 + b), pb(bank[h, k], 0, b - a), AF.Relu, bias=-2048.0,
+                scale=512.0, accum=v("ct", 32 * k + h, 32 * k + h + 1))
+
+        def lifted(h, k):
+            a, b = RUNS[k]
+            ts(v("ta", C * h + a, C * h + b), v("tb", TBW * h + 1 + a, TBW * h + 1 + b), 513.0 / 512, None, ALU.mult)
+
+        for k in range(2):
+            for h in range(2):
+                match(h, k)
+        lifted(0, 0)
+        lifted(1, 0)
+        for b in range(1, 4):
+            held(b)
+        mm(4, "skq", "skp", 0, "bq", "bp", 0, C)
+        for b in range(1 if r else 0, 4):
+            act(v("dh", C * b, C * b + C), pb(b, 0, C), AF.Copy)
+        if r == 0:
+            act(v("nb"), v("ones", 0, 32), AF.Copy, scale=-1e29)
+            act(v("dc", 2, 4), v("dc", 0, 2), AF.Copy, scale=0.5)
+            act(v("dc", 4, 6), v("dc", 0, 2), AF.Copy, scale=-0.5)
+        tr(v("ctt"), v("ct"))
+        lifted(0, 1)
+        scan(v("ci", 1, 33), v("ctt", 0, 32), v("ctt", 32, 64), 0.0, ALU.add, ALU.add)
+        lifted(1, 1)
+        tr(v("bx"), v("ci", 0, 32))
+        if r == 0:
+            cp(v("rb", 479, 512, 32), v("dum"))
+        ts(v("bxs"), v("bx", 0, 2), 1.0 / 512, None, ALU.mult)
+        if r == 0:
+            cp(v("rb", 991, 1024, 32), v("dum"))
+        for h in range(2):
+            scan(v("zs", C * h, C * h + C), v("ta", C * h, C * h + C), v("tb", TBW * h, TBW * h + C),
+                 v("bxs", h, h + 1), ALU.add, ALU.subtract)
+        for h in range(2):
+            tr(v("zt", C * h, C * h + C), v("zs", C * h, C * h + C))
+        for h in range(2):
+            scan(v("rb", 512 * h, 512 * h + C), v("mr"), v("zt", C * h, C * h + C), 0.0, ALU.mult, ALU.max)
+        tr(v("wt"), v("rb", 31, 1024, 32))
+        if r == 0:
+            ts(v("corr"), v("dmf", 15, 16), 1.0, 512.0, ALU.min, ALU.mult)
+        ts(v("wo"), v("wt"), 513.0, None, ALU.subtract)
+        scatter(v("sw"), v("wo"), v("jv"))
+        scan(v("wr"), v("mw"), v("sw", 0, C), 0.0, ALU.add, ALU.max)
+        ts(v("lo"), v("wr", 15, C, 16), v("corr"), float(HC), ALU.subtract, ALU.add)
+        for c in range(4):
+            act(v("gs", C * c, C * c + C), pb(4, 0, C), AF.Sign, bias=v("th", c, c + 1), accum=v("s4", c, c + 1))
+        for c in range(2):
+            act(v("eb", c, c + 1), v("s4", c, c + 1), AF.Identity, bias=v("dc", c, c + 1), scale=v("dc", 4 + c, 5 + c))
+        act(v("se"), v("s4"), AF.Identity, bias=float(HC), scale=-0.5)
+        for c in range(2):
+            act(v("ed", c, c + 1), v("s4", 2 + c, 3 + c), AF.Relu, bias=v("eb", c, c + 1), scale=v("dc", 2 + c, 3 + c))
+
+        def sorted_part(b, a, n):
+            return v("gs", C * b + a, C * b + a + n), ind(v("dh", C * b, C * b + C), v("lo", a // 16, (a + n) // 16))
+
+        def running(b):
+            scan(v("oo", OW * b + 1, OW * b + 1 + C), v(mmr, 0, C), v("gs", C * b, C * b + C), 0.0, ALU.add, ALU.max)
+
+        def ends(b):
+            return v("at", b, 128, 4), ind(v("oo", OW * b, OW * b + C + 33), v("so", 2, 4))
+
+        act(*sorted_part(1, 0, C), AF.Copy)
+        cp(*sorted_part(0, 0, C))
+        for c in range(2):
+            ts(v("so", c, 4, 2), v("se", c, 4, 2), v("ed", c, c + 1), None, ALU.max)
+        act(*sorted_part(2, 0, C), AF.Copy)
+        cp(*sorted_part(3, CUT, C - CUT))
+        scatter(v(mmr), v("so", 0, 2), v("nb"))
+        act(*sorted_part(3, 0, CUT), AF.Copy)
+        for b in range(4):
+            running(b)
+            if b < 3:
+                act(*ends(b), AF.Copy, scale=2.0)
+        ts(*ends(3), 2.0, None, ALU.mult)
+        quant(lq, lp, 96, 224, v("at"))
+
+        def send(buf, code, r=r):
+            src = v(buf, 96, 128)
+            ids, dsts = [], []
+            for k in others:
+                slot = [j for j in range(n_ranks) if j != k].index(rank)
+                d = v(buf, M * slot, M * slot + M)
+                rid, pid, _ = topo.addr(cores[k])
+                ids.append(DstId(rid=int(rid), pnc=int(pid)))
+                dsts.append(as_bytes(d)[0] if code else d[0])
+            s = as_bytes(src)[0] if code else src[0]
+            add("g", "r", lambda: g.remote_dma_fused(
+                [RemoteDMATransfer(dst_ids=ids, dma_engine_mask=mask, remote_sem=T.sem["arr%d" % r],
+                                   srcs=[s], dsts=dsts)], local_sem=T.sem.sent), [src], [])
+        send(lq, True)
+        send(lp, False)
+        ops.append(dict(q=None, kind="x", sem="arr%d" % r, n=2 * n_eng * len(others), r=[],
+                        w=foot([v(lq, 0, 96), v(lp, 0, 96)])))
+
+        act(v(kf), pb(4, 0, C), AF.Identity, bias=15.5)
+        if r == 0:
+            for b in range(4):
+                unit("e1q", "e1p", "f1", b)
+        dma("s", T.kl[8 * r:8 * r + 8, :], (T[kf][0:128:16, :], v(kf)[1]))
+        scan(v("kr"), v("mw"), v(kf), 0.0, ALU.add, ALU.max)
+        ts(v("ko"), v("kr", 15, C, 16), v("corr"), None, ALU.subtract)
+        if r == 0:
+            zeros(v("zz", 128, 512))
+            zeros(v("gt", 128, 512))
+            zeros(v("mm1"))
+        else:
+            quant("vq", "vp", 0, 128, v("vs"))
+
+        for b in range(4):
+            mm(4 + b, "e1q", "e1p", 128 * b, lq, lp, 0, 128)
+        for b in range(4):
+            act(v("ya", 64 * b, 64 * b + 64), pb(4 + b, 64, 128), AF.Copy)
+            tt(v("y2", b, 256, 4), pb(4 + b, 0, 64), v("ya", 64 * b, 64 * b + 64), ALU.max)
+        tt(v("zz", 0, 128), v("y2", 0, 128), v("y2", 128, 256), ALU.max)
+        quant("zq", "zp", 0, 128, v("zz"))
+        for b in range(4):
+            mm(4 + b, "wq", "wp", 128 * b, "zq", "zp", 0, 128)
+        for b in range(4):
+            if b % 2 == 0:
+                act(v("gt", b, 128, 4), pb(4 + b, 0, M), AF.Relu, scale=0.015625)
+            else:
+                ts(v("gt", b, 128, 4), pb(4 + b, 0, M), 0.0, 0.015625, ALU.max, ALU.mult)
+        quant("gq", "gp", 0, 128, v("gt"))
+        order = (0, 2, 1, 3)
+        for k, b in enumerate(order):
+            mm(4 + k, "ehq", "ehp", 128 * b, "gq", "gp", 0, 128)
+
+        new = "st%d" % (r + 1)
+        go = first_products(r + 1)
+
+        def part(b, half):
+            a, e = RUNS[half]
+            return (v(new, 4 * a + b, 4 * e, 4), ind(v("gw", M * b, M * b + M), v("ko", a // 16, e // 16)),
+                    v("dh", C * b + a, C * b + e), pb(b, a, e))
+
+        for k, b in enumerate(order):
+            if k == 0:
+                cp(v("gw", M * b, M * b + M), pb(4 + k, 0, M))
+            else:
+                act(v("gw", M * b, M * b + M), pb(4 + k, 0, M), AF.Copy)
+        tmp = {}
+        for b in (2, 3):
+            tmp[b] = v("tm", CUT * (b - 2), CUT * (b - 1))
+            act(tmp[b], part(b, 0)[1], AF.Copy)
+        for b in (0, 1):
+            o, gath, d, _ = part(b, 0)
+            tt(o, gath, d, ALU.add)
+        for b in tmp:
+            o, _, _, dp = part(b, 0)
+            tt(o, tmp[b], dp, ALU.add)
+        go(0)
+        n = C - CUT
+        for b in range(4):
+            late = v("tm", 2 * CUT + n * b, 2 * CUT + n * b + n)
+            o, gath, _, dp = part(b, 1)
+            act(late, gath, AF.Copy)
+            tt(o, late, dp, ALU.add)
+        go(1)
+
+    last = "xp%d" % ROUNDS
+    act(v("yf", 0, CUT), pb(4, 0, CUT), AF.Copy)
+    cp(v("yf", CUT, C), pb(5, 0, C - CUT))
+    dma("a", T.y[:, 0:CUT], v("yf", 0, CUT))
+    dma("s", T.y[:, CUT:C], v("yf", CUT, C))
+    for k in range(4):
+        dma("a", T.osc[4 * k:4 * k + 4, :], (T[last][32 * k:32 * k + 4, :], v(last)[1]))
+
+    count = {"v": 0, "a": 0, "t": 0, "g": 0}
+    known = {q: {} for q in eng}
+    n_dma, sent = 0, 0
+    log = {}
+    for i, op in enumerate(ops):
+        q = op["q"]
+        need = set()
+        for name, cols in op["r"]:
+            for j, jq, jc, jw in log.get(name, []):
+                if (jw or (name.startswith("pb") and jq != q)) and not cols.isdisjoint(jc):
+                    need.add(j)
+        for name, cols in op["w"]:
+            for j, jq, jc, jw in log.get(name, []):
+                if not cols.isdisjoint(jc):
+                    need.add(j)
+        for name, cols in op["r"]:
+            log.setdefault(name, []).append((i, q, cols, False))
+        for name, cols in op["w"]:
+            log.setdefault(name, []).append((i, q, cols, True))
+        if op["kind"] == "x":
+            op["tok"], op["clock"] = (op["sem"], op["n"]), {op["sem"]: op["n"]}
+            continue
+        mine = known[q]
+        for j in sorted(need, reverse=True):
+            sem, n = ops[j]["tok"]
+            if mine.get(sem, 0) < n:
+                eng[q].wait_ge(T.sem[sem], n)
+                for s2, n2 in ops[j]["clock"].items():
+                    mine[s2] = max(mine.get(s2, 0), n2)
+        ins = op["fn"]()
+        if op["kind"] == "c":
+            count[q] += 1
+            op["tok"] = ("q" + q, count[q])
+            ins.then_inc(T.sem["q" + q], 1)
+        elif op["kind"] == "d":
+            op["tok"] = ("d%d" % n_dma, 16)
+            ins.then_inc(T.sem["d%d" % n_dma], 16)
+            n_dma += 1
+        else:
+            sent += n_eng
+            op["tok"] = ("sent", sent)
+        op["clock"] = dict(mine)
+        op["clock"][op["tok"][0]] = op["tok"][1]
+    g.wait_ge(T.sem.sent, sent)
+    for q in count:
+        g.wait_ge(T.sem["q" + q], count[q])
+    for k in range(n_dma):
+        g.wait_ge(T.sem["d%d" % k], 16)

@@ -1,26 +1,29 @@
 from concourse.bass import DstId, RemoteDMATransfer
-from concourse.mybir import dt, AluOpType, AxisListType, ActivationFunctionType
+from concourse.mybir import dt, AluOpType, ActivationFunctionType
 
 ALU = AluOpType
 AF = ActivationFunctionType
 C, HC, M, ROUNDS = 448, 224, 32, 2
-CUT = 320
-RUNS = ((0, CUT), (CUT, C))
 F16 = "float16"
 OW = 496
 TBW = 464
 BF, F32, I32, U16, CODE, PLANE = "bfloat16", "float32", "int32", "uint16", "float8_e4m3fn_x4", "uint8"
 
+CUTS = ((128, 320), (256,), (256,))
+COUNT_CUTS = ((320,), (256,))
+FUSED = ((0, 0, 256), (1, 0, 256), (0, 256, 448))
+PIECES = ((2, 0, 256), (3, 0, 256), (1, 256, 448), (2, 256, 448), (3, 256, 448))
+SORT_VECTOR = ((0, 0, 448), (3, 256, 448))
+SORT_SCALAR = ((1, 0, 448), (2, 0, 448), (3, 0, 256))
+
 WIDTHS = {
-    BF: dict(st0=4 * C, st1=4 * C, st2=4 * C, us=512, vs=512, ones=516, f1=516, fh=516, bt=4 * C, stt=1024,
-             stk=512, bs=128, mw=C, mr=C, tb=2 * TBW, jv=512, sw=704, dh=4 * C, gs=4 * C, oo=4 * OW + 16,
-             mm0=OW, mm1=OW, nb=32, at=512, ya=256, y2=256, zz=512, gt=512, gw=128,
-             tm=2 * CUT + 4 * (C - CUT)),
-    F32: dict(tf=32, sig=32, mwf=128, rf=32, wk0=32, wks=1, wk=1, dmf=16, m16a=16, m16b=16, cst=6, th=4,
-              dc=6, ndm=1, corr=1, dum=2, ct=64, ctt=64, ci=40, bx=32, bxs=2, s4=4, se=4, eb=2, ed=2,
-              kf0=C, kf1=C, yf=C),
-    I32: dict(pi=1, ti=5, mwi=128, mwj=128, dmi=16, dmj=16),
-    F16: dict(ta=2 * C, zs=2 * C, zt=2 * C, rb=1024, wt=32, wr=C, kr=C),
+    BF: dict(st0=4 * C, st1=4 * C, st2=4 * C, us=512, vs=512, ones=512, hf=516, f1=516, fh=516, bt=4 * C, stt=1024,
+             stk=512, tf=256, tk=128, mk=16, mw=C, hr=34, tb=2 * TBW, jv=512, sw=704, dh=4 * C, gs=4 * C,
+             oo=4 * OW + 16, mm0=OW, mm1=OW, nb=32, at=512, ya=256, y2=256, gw=128, tm=4 * C),
+    F32: dict(sg=4, dmf=16, m16a=16, m16b=16, cst=2, dc=2, ndm=1, corr=1, odd=1, dum=2, cc=6, junk=18, rw=3, hd=1,
+              zj=2, zi=2, ci=32, bx=32, se=3, ed=2, kf0=C, kf1=C, yf=C),
+    I32: dict(pi=4, ti=4, dmi=16, dmj=16),
+    F16: dict(ta=2 * C, zs=2 * C, zt=2 * C, rb=2 * C, cb=HC, ct=HC, rr=32, wt=32, wr=C, kr=C),
     U16: dict(wo=32, lo=28, so=4, ko=28),
     CODE: dict(xq0=C, xq1=C, xq2=C, uq=128, vq=128, wq=512, ehq=512, e1q=512, bq=C, stq=256, skq=128,
                lq0=224, lq1=224, zq=128, gq=128),
@@ -33,7 +36,7 @@ for _dtype, _bufs in WIDTHS.items():
         SCRATCH[_name] = ("sbuf", [128, _w], _dtype)
 for _k in range(8):
     SCRATCH["pb%d" % _k] = ("psum", [128, 512], F32)
-NDMA = 20
+NDMA = 17
 SEMAPHORES = ["qv", "qa", "qt", "qg", "sent", "arr0", "arr1"] + ["d%d" % _k for _k in range(NDMA)]
 
 
@@ -51,10 +54,10 @@ def rank_program(g, core, T, topo):
             b = SCRATCH[name][1][1]
         ap = T[name][:, a:b] if s == 1 else T[name][:, a:b:s]
         cols = frozenset([0]) if name.startswith("pb") else frozenset(range(a, b, s))
-        return (ap, [(name, cols)])
+        return (ap, [(name, cols)], len(range(a, b, s)))
 
     def ind(win, off):
-        return (win[0].indirect(off[0]), win[1] + off[1])
+        return (win[0].indirect(off[0]), win[1] + off[1], 16 * off[2])
 
     def ap(x):
         return x[0] if isinstance(x, tuple) else x
@@ -103,8 +106,7 @@ def rank_program(g, core, T, topo):
             kw["scale"] = ap(scale)
         if accum is not None:
             kw["accum_out"] = ap(accum)
-        add("a", "c", lambda: g.scalar.activation(ap(out), ap(in_), func, **kw), [in_, bias, scale],
-            [out, accum])
+        add("a", "c", lambda: g.scalar.activation(ap(out), ap(in_), func, **kw), [in_, bias, scale], [out, accum])
 
     def mm(bank, lq, lp, la, rq, rp, a, b):
         sides = [v(lq, la, la + 128), v(lp, la, la + 128), v(rq, a, b), v(rp, a, b)]
@@ -123,7 +125,7 @@ def rank_program(g, core, T, topo):
                 [], [out])
 
     def zeros(out):
-        iota(out, [[0, len(out[1][0][1])]], 0, 0)
+        iota(out, [[0, out[2]]], 0, 0)
 
     def sel(out, in_, pattern, op, fill, base, cm):
         add("g", "c", lambda: g.affine_select(ap(out), ap(in_), pattern, op, fill, base, cm), [in_], [out])
@@ -132,94 +134,111 @@ def rank_program(g, core, T, topo):
         add(q, "d", lambda: eng[q].dma_start(ap(out), ap(in_)), [in_] + list(after), [out])
 
     def as_bytes(x):
-        return (x[0].bitcast(dt.uint8), x[1])
+        return (x[0].bitcast(dt.uint8),) + x[1:]
 
-    dma("s", v("st0", 0, 4 * CUT), T.x[:, 0:4 * CUT])
+    def pieces(cuts):
+        edges = (0,) + tuple(cuts) + (C,)
+        return list(zip(edges, edges[1:]))
+
     dma("s", v("us"), T.u[:, :])
-    dma("s", v("st0", 4 * CUT, 4 * C), T.x[:, 4 * CUT:4 * C])
+    for a, b in pieces(CUTS[0]):
+        dma("s", v("st0", 4 * a, 4 * b), T.x[:, 4 * a:4 * b])
     dma("s", as_bytes(v("wq")), T.wc[:, :], after=[v("st0")])
-    dma("s", v("wp"), T.ws[:, :])
-    dma("s", v("vs"), T.v[:, :])
+    dma("s", v("wp"), T.ws[:, :], after=[v("st0")])
+    dma("s", v("vs"), T.v[:, :], after=[v("st0")])
 
-    iota(v("pi"), [[0, 1]], 0, 1, True)
-    iota(v("mwi"), [[-16, 8], [0, 16]], 128, 1, True)
     mset(v("ones"), 1.0)
+    for i in range(4):
+        iota(v("pi", i, i + 1), [[0, 1]], 0, 8 >> i, True)
+    ts(v("ti"), v("pi"), 3, 1, ALU.logical_shift_right, ALU.bitwise_and)
+    ts(v("sg"), v("ti"), 2.0, -1.0, ALU.mult, ALU.add)
+    sel(v("mk"), v("ones", 0, 16), [[0, 2], [-16, 8]], ALU.is_ge, 0.0, 0, 1)
+    sel(v("mk"), v("mk"), [[0, 2], [16, 8]], ALU.is_ge, 0.0, 15, -1)
     mset(v("tf"), 0.0)
-    iota(v("dmi"), [[1, 16]], 128, -1, True)
-    iota(v("rf"), [[1, 32]], 0, 0)
-    sel(v("f1"), v("ones"), [[1, 516]], ALU.is_equal, 0.0, -3, -4)
-    iota(v("cst", 0, 4), [[-1, 2], [-16, 2]], 1, 0)
-    iota(v("cst", 4, 6), [[16, 2]], C + 16, 0)
-    zeros(v("tb", 0, 2 * TBW, TBW))
-    zeros(v("ct"))
-    zeros(v("ci", 0, 1))
-    iota(v("dum"), [[128, 2]], 513 + C, 1)
-    sel(v("mr"), v("ones", 0, C), [[0, 14], [1, 32]], ALU.is_gt, 0.0, 0, 0)
-    iota(v("jv"), [[1, 32], [32, 16]], -HC, 0)
-
-    for k in range(2):
-        act(v("bt", 512 * k, 512 * k + 512), v("ones", 0, 512), AF.Copy, scale=0.0)
-    for i in range(5):
-        ts(v("ti", i, i + 1), v("pi"), i, 1, ALU.logical_shift_right, ALU.bitwise_and)
-    ts(v("mwj"), v("mwi"), 4, None, ALU.logical_shift_right)
-    ts(v("tf", 0, 5), v("ti"), 2.0, -1.0, ALU.mult, ALU.add)
-    ts(v("tf", 16, 21), v("ti"), 2.0, -1.0, ALU.mult, ALU.add)
-    ts(v("mwf"), v("mwj"), 8.0, None, ALU.is_equal)
-    tr(v("sig"), v("tf"))
-    mset(v("bt", 1024, 4 * C), 0.0)
-    for t in range(4):
-        act(v("bs", t, 128, 4), v("sig"), AF.Copy)
-    ts(v("dmj"), v("dmi"), 15, None, ALU.bitwise_and)
-    tt(v("wk0"), v("sig"), v("rf"), ALU.mult)
-    cp(v("dmf"), v("dmj"))
-    add("v", "c", lambda: g.vector.tensor_reduce(T.wks[:, 0:1], T.wk0[:, :], AxisListType.X, ALU.add),
-        [v("wk0")], [v("wks")])
+    for i in range(4):
+        act(v("tf", i, 256, 16), v("mk"), AF.Copy, scale=v("sg", i, i + 1))
     for h in range(2):
-        for a in range(4):
-            dst, col = v("stt", 512 * h + 128 * a, 512 * h + 128 * a + 128), 16 * (2 * a + h)
-            if a < 2:
-                act(dst, v("bs"), AF.Copy, scale=v("mwf", col, col + 1))
-            else:
-                ts(dst, v("bs"), v("mwf", col, col + 1), None, ALU.mult)
+        act(v("tf", 128 * h + 4, 128 * h + 128, 16), v("mk", 0, 8), AF.Copy, scale=2.0 * h - 1.0)
+    mset(v("stt", 0, 512), 0.0)
+    act(v("stt", 512, 1024), v("ones"), AF.Copy, scale=0.0)
+    tr(v("stt", 0, 1024, 4), v("tf"))
     quant("stq", "stp", 0, 256, v("stt"))
-    act(v("wk"), v("wks"), AF.Copy, scale=1.0 / 32)
-    act(v("fh"), v("f1"), AF.Copy, scale=0.5)
-    for t in range(4):
-        act(v("stk", t, 512, 4), v("mwf"), AF.Copy, scale=v("wk"))
-
-    def unit(q, p, src, b):
-        quant(q, p, 128 * b, 128 * b + 128, v(src, 3 - b, 515 - b))
-
-    def first_products(r):
-        def go(half):
-            a, b = RUNS[half]
-            quant("xq%d" % r, "xp%d" % r, a, b, v("st%d" % r, 4 * a, 4 * b))
-            if r == 0 and half == 0:
-                quant("uq", "up", 0, 128, v("us"))
-            if r < ROUNDS:
-                mm(4 + half, "uq", "up", 0, "xq%d" % r, "xp%d" % r, a, b)
-            else:
-                mm(4 + half, "vq", "vp", 0, "xq%d" % r, "xp%d" % r, a, b)
-                dma("s", T.oc[:, 4 * a:4 * b], as_bytes(v("xq%d" % r, a, b)))
-        return go
-
-    go = first_products(0)
-    go(0)
+    for a, b in pieces(CUTS[0])[:2]:
+        mset(v("bt", 4 * a, 4 * b), 0.0)
+    act(v("bt", 4 * C - 512, 4 * C), v("ones"), AF.Copy, scale=0.0)
+    mset(v("hf"), 0.5)
+    sel(v("fh"), v("hf"), [[1, 516]], ALU.is_equal, 0.0, -3, -4)
+    iota(v("dmi"), [[1, 16]], 128, -1, True)
+    ts(v("dmj"), v("dmi"), 15, None, ALU.bitwise_and)
+    cp(v("dmf"), v("dmj"))
+    iota(v("cst"), [[16, 2]], C + 16, 0)
+    act(v("ndm"), v("dmf", 15, 16), AF.Copy, scale=-1.0)
+    act(v("dc"), v("cst"), AF.Identity, bias=v("ndm"))
+    zeros(v("tb", 0, 2 * TBW, TBW))
+    iota(v("dum"), [[128, 2]], C - 511, 1)
+    for hg in range(2):
+        act(v("rr", 16 * hg + 14, 16 * hg + 16), v("dum"), AF.Copy)
+    act(v("junk", 0, 4), v("mk", 1, 8, 2), AF.Identity, scale=float(C), bias=C / 4.0, accum=v("odd"))
+    ts(v("zj"), v("dmf", 0, 16, 15), 0.0, -1024.0, ALU.is_equal, ALU.mult)
+    act(v("hd"), v("zj", 0, 1), AF.Identity, bias=v("zj", 1, 2))
+    act(v("zi", 0, 1), v("zj", 0, 1), AF.Identity, scale=-1.0, bias=1.0)
+    act(v("zi", 1, 2), v("zj", 1, 2), AF.Copy)
+    iota(v("hr"), [[0, 34]], 1024, 0)
+    sel(v("hr", 1, 33), v("hr", 1, 33), [[0, 2], [1, 16]], ALU.is_gt, 0.0, -13, 0)
+    iota(v("jv"), [[1, 32], [32, 16]], -HC, 0)
     ts(v("m16a"), v("dmf"), 0.0, -4096.0, ALU.is_equal, ALU.mult)
     ts(v("m16b"), v("dmf"), 1.0, 512.0, ALU.is_equal, ALU.mult)
-    quant("skq", "skp", 0, 128, v("stk"))
     tt(v("mw", 0, 16), v("m16a"), v("m16b"), ALU.add)
-    go(1)
     w = 16
     while w < C:
         n = min(w, C - w)
-        sel(v("mw", w, w + n), v("mw", 0, n), [[0, n]], ALU.is_ge, 0.0, 0, 0)
+        act(v("mw", w, w + n), v("mw", 0, n), AF.Copy)
         w += n
+    ts(v("corr"), v("dmf", 15, 16), 1.0, 512.0, ALU.min, ALU.mult)
+    act(v("nb"), v("ones", 0, 32), AF.Copy, scale=-1e29)
     zeros(v("mm0"))
     zeros(v("oo", 0, 1))
     for b in range(4):
         zeros(v("oo", OW * b + C + 1, OW * (b + 1) + 1))
     zeros(v("at", 128, 512))
+    zeros(v("tk"))
+    zeros(v("stk"))
+
+    def unit(q, p, src, b):
+        quant(q, p, 128 * b, 128 * b + 128, v(src, 3 - b, 515 - b))
+
+    for b in range(4):
+        unit("ehq", "ehp", "fh", b)
+
+    def first_products(r, k):
+        rn = pieces(CUTS[r])
+        a, b = rn[k]
+        xq, xp, at = "xq%d" % r, "xp%d" % r, 4 + k % 2
+        quant(xq, xp, a, b, v("st%d" % r, 4 * a, 4 * b))
+        if r == ROUNDS:
+            mm(at, "vq", "vp", 0, xq, xp, a, b)
+            dma("s", T.oc[:, 4 * a:4 * b], as_bytes(v(xq, a, b)))
+            if k == 0:
+                act(v("yf", a, b), pb(at, 0, b - a), AF.Copy)
+            else:
+                cp(v("yf", a, b), pb(at, 0, b - a))
+            dma("as"[k], T.y[:, a:b], v("yf", a, b))
+            return
+        mm(at, "uq", "up", 0, xq, xp, a, b)
+        act(v("bt", 4 * a, 4 * b, 4), pb(at, 0, b - a), AF.Sign, bias=-1e-36)
+        quant("bq", "bp", a, b, v("bt", 4 * a, 4 * b))
+        final = k == len(rn) - 1
+        for h in range(2):
+            bank, n = (4 if final else 6) + h, 2 * k + h
+            mm(bank, "stq", "stp", 128 * h, "bq", "bp", a, b)
+            act(v("tb", TBW * h + 1 + a, TBW * h + 1 + b), pb(bank, 0, b - a), AF.Relu, bias=-2048.0,
+                scale=512.0, accum=v("cc", n, n + 1))
+            ts(v("ta", C * h + a, C * h + b), v("tb", TBW * h + 1 + a, TBW * h + 1 + b),
+               (513.0 if h else 511.0) / 512, None, ALU.mult)
+
+    quant("uq", "up", 0, 128, v("us"))
+    for k in range(len(CUTS[0]) + 1):
+        first_products(0, k)
 
     others = [k for k in range(n_ranks) if k != rank]
     mask = topo.mask(core, cores[others[0]])
@@ -229,103 +248,55 @@ def rank_program(g, core, T, topo):
 
     for r in range(ROUNDS):
         xq, xp, lq, lp, mmr, kf = ["%s%d" % (s, r) for s in ("xq", "xp", "lq", "lp", "mm", "kf")]
-
-        def held(b):
+        nk = len(CUTS[r]) + 1
+        for b in range(4):
             mm(b, "ehq", "ehp", 128 * b, xq, xp, 0, C)
-
-        bank = {(0, 0): 6, (1, 0): 7, (0, 1): 4, (1, 1): 5}
-        for k, (a, b) in enumerate(RUNS):
-            act(v("bt", 4 * a, 4 * b, 4), pb(4 + k, 0, b - a), AF.Sign, bias=-1e-36)
-            quant("bq", "bp", a, b, v("bt", 4 * a, 4 * b))
-        if r:
-            held(0)
-            cp(v("dh", 0, C), pb(0, 0, C))
-        else:
-            act(v("ndm"), v("dmf", 15, 16), AF.Copy, scale=-1.0)
-            act(v("th"), v("cst", 0, 4), AF.Identity, bias=v("dmf", 15, 16))
-            act(v("dc", 0, 2), v("cst", 4, 6), AF.Identity, bias=v("ndm"))
-        for k, (a, b) in enumerate(RUNS):
-            for h in range(2):
-                mm(bank[h, k], "stq", "stp", 128 * h, "bq", "bp", a, b)
-        if r == 0:
-            for b in range(4):
-                unit("ehq", "ehp", "fh", b)
-            held(0)
-
-        def match(h, k):
-            a, b = RUNS[k]
-            act(v("tb", TBW * h + 1 + a, TBW * h + 1 + b), pb(bank[h, k], 0, b - a), AF.Relu, bias=-2048.0,
-                scale=512.0, accum=v("ct", 32 * k + h, 32 * k + h + 1))
-
-        def lifted(h, k):
-            a, b = RUNS[k]
-            ts(v("ta", C * h + a, C * h + b), v("tb", TBW * h + 1 + a, TBW * h + 1 + b), 513.0 / 512, None, ALU.mult)
-
-        for k in range(2):
-            for h in range(2):
-                match(h, k)
-        lifted(0, 0)
-        lifted(1, 0)
-        for b in range(1, 4):
-            held(b)
-        mm(4, "skq", "skp", 0, "bq", "bp", 0, C)
-        for b in range(1 if r else 0, 4):
             act(v("dh", C * b, C * b + C), pb(b, 0, C), AF.Copy)
-        if r == 0:
-            act(v("nb"), v("ones", 0, 32), AF.Copy, scale=-1e29)
-            act(v("dc", 2, 4), v("dc", 0, 2), AF.Copy, scale=0.5)
-            act(v("dc", 4, 6), v("dc", 0, 2), AF.Copy, scale=-0.5)
-        tr(v("ctt"), v("ct"))
-        lifted(0, 1)
-        scan(v("ci", 1, 33), v("ctt", 0, 32), v("ctt", 32, 64), 0.0, ALU.add, ALU.add)
-        lifted(1, 1)
-        tr(v("bx"), v("ci", 0, 32))
-        if r == 0:
-            cp(v("rb", 479, 512, 32), v("dum"))
-        ts(v("bxs"), v("bx", 0, 2), 1.0 / 512, None, ALU.mult)
-        if r == 0:
-            cp(v("rb", 991, 1024, 32), v("dum"))
         for h in range(2):
-            scan(v("zs", C * h, C * h + C), v("ta", C * h, C * h + C), v("tb", TBW * h, TBW * h + C),
-                 v("bxs", h, h + 1), ALU.add, ALU.subtract)
+            act(v("junk", 6 * h, 6 * h + nk), v("cc", h, 2 * nk, 2), AF.Copy, scale=1.0 / 512, accum=v("rw", h, h + 1))
+            act(v("ed", h, h + 1), v("rw", h, h + 1), AF.Relu, bias=v("dc", h, h + 1), scale=-512.0)
+        act(v("junk", 12, 12 + 2 * nk), v("cc", 0, 2 * nk), AF.Copy, scale=1.0 / 512, accum=v("rw", 2, 3))
+        act(v("cb"), v("ones", 0, HC), AF.Identity, scale=v("hd"), bias=v("rw", 2, 3))
+        tr(v("ct"), v("cb"))
+        scan(v("ci"), v("ct", 0, 32), v("hr", 0, 32), 0.0, ALU.add, ALU.add)
+        tr(v("bx"), v("ci"))
+        act(v("se", 0, 1), v("bx", 0, 1), AF.Identity, scale=-1.0, bias=v("odd"))
+        for c in range(2):
+            act(v("se", c + 1, c + 2), v("rw", 1 - c, 2 - c), AF.Identity, bias=v("se", c, c + 1))
         for h in range(2):
-            tr(v("zt", C * h, C * h + C), v("zs", C * h, C * h + C))
-        for h in range(2):
-            scan(v("rb", 512 * h, 512 * h + C), v("mr"), v("zt", C * h, C * h + C), 0.0, ALU.mult, ALU.max)
-        tr(v("wt"), v("rb", 31, 1024, 32))
-        if r == 0:
-            ts(v("corr"), v("dmf", 15, 16), 1.0, 512.0, ALU.min, ALU.mult)
-        ts(v("wo"), v("wt"), 513.0, None, ALU.subtract)
+            for a, e in pieces(COUNT_CUTS[r]):
+                scan(v("zs", C * h + a, C * h + e), v("ta", C * h + a, C * h + e), v("tb", TBW * h + a, TBW * h + e),
+                     v("zs", C * h + a - 1, C * h + a) if a else v("zi", h, h + 1), ALU.add, ALU.subtract)
+                tr(v("zt", C * h + a, C * h + e), v("zs", C * h + a, C * h + e))
+            for a in (0, HC):
+                if h:
+                    scan(v("rb", C + a, C + a + HC), v("ct"), v("zt", C + a, C + a + HC), 0.0, ALU.add, ALU.max)
+                else:
+                    scan(v("rb", a, a + HC), v("zt", a, a + HC), v("ct"), -2048.0, ALU.max, ALU.add)
+        for hg in range(2):
+            tt(v("rr", 16 * hg, 16 * hg + 14), v("rb", 16 * hg + 15, C, 32), v("rb", C + 16 * hg + 15, 2 * C, 32),
+               ALU.max)
+        tr(v("wt"), v("rr"))
+        ts(v("wo"), v("wt"), 511.0, None, ALU.add)
         scatter(v("sw"), v("wo"), v("jv"))
         scan(v("wr"), v("mw"), v("sw", 0, C), 0.0, ALU.add, ALU.max)
         ts(v("lo"), v("wr", 15, C, 16), v("corr"), float(HC), ALU.subtract, ALU.add)
-        for c in range(4):
-            act(v("gs", C * c, C * c + C), pb(4, 0, C), AF.Sign, bias=v("th", c, c + 1), accum=v("s4", c, c + 1))
         for c in range(2):
-            act(v("eb", c, c + 1), v("s4", c, c + 1), AF.Identity, bias=v("dc", c, c + 1), scale=v("dc", 4 + c, 5 + c))
-        act(v("se"), v("s4"), AF.Identity, bias=float(HC), scale=-0.5)
-        for c in range(2):
-            act(v("ed", c, c + 1), v("s4", 2 + c, 3 + c), AF.Relu, bias=v("eb", c, c + 1), scale=v("dc", 2 + c, 3 + c))
+            ts(v("so", c, 4, 2), v("se", 1 - c, 3 - c), v("ed", c, c + 1), None, ALU.max)
+        scatter(v(mmr), v("so", 0, 2), v("nb"))
 
-        def sorted_part(b, a, n):
-            return v("gs", C * b + a, C * b + a + n), ind(v("dh", C * b, C * b + C), v("lo", a // 16, (a + n) // 16))
-
-        def running(b):
-            scan(v("oo", OW * b + 1, OW * b + 1 + C), v(mmr, 0, C), v("gs", C * b, C * b + C), 0.0, ALU.add, ALU.max)
+        def sorted_part(b, a, e):
+            return v("gs", C * b + a, C * b + e), ind(v("dh", C * b, C * b + C), v("lo", a // 16, e // 16))
 
         def ends(b):
             return v("at", b, 128, 4), ind(v("oo", OW * b, OW * b + C + 33), v("so", 2, 4))
 
-        act(*sorted_part(1, 0, C), AF.Copy)
-        cp(*sorted_part(0, 0, C))
-        for c in range(2):
-            ts(v("so", c, 4, 2), v("se", c, 4, 2), v("ed", c, c + 1), None, ALU.max)
-        act(*sorted_part(2, 0, C), AF.Copy)
-        cp(*sorted_part(3, CUT, C - CUT))
-        scatter(v(mmr), v("so", 0, 2), v("nb"))
-        act(*sorted_part(3, 0, CUT), AF.Copy)
+        for piece in SORT_SCALAR:
+            act(*sorted_part(*piece), AF.Copy)
+        for piece in SORT_VECTOR:
+            cp(*sorted_part(*piece))
         for b in range(4):
-            running(b)
+            scan(v("oo", OW * b + 1, OW * b + 1 + C), v(mmr, 0, C), v("gs", C * b, C * b + C), 0.0, ALU.add, ALU.max)
             if b < 3:
                 act(*ends(b), AF.Copy, scale=2.0)
         ts(*ends(3), 2.0, None, ALU.mult)
@@ -346,85 +317,67 @@ def rank_program(g, core, T, topo):
                                    srcs=[s], dsts=dsts)], local_sem=T.sem.sent), [src], [])
         send(lq, True)
         send(lp, False)
-        ops.append(dict(q=None, kind="x", sem="arr%d" % r, n=2 * n_eng * len(others), r=[],
+        ops.append(dict(q="x", kind="x", sem="arr%d" % r, n=2 * n_eng * len(others), r=[],
                         w=foot([v(lq, 0, 96), v(lp, 0, 96)])))
 
-        act(v(kf), pb(4, 0, C), AF.Identity, bias=15.5)
         if r == 0:
+            for i in range(5):
+                act(v("tk", i, 128, 16), v("mk", 0, 8), AF.Copy, scale=2.0 ** (i - 1))
+            act(v("mm1"), v("ones", 0, OW), AF.Copy, scale=0.0)
+            tr(v("stk", 0, 512, 4), v("tk"))
+            quant("skq", "skp", 0, 128, v("stk"))
+            act(v("f1"), v("fh"), AF.Copy, scale=2.0)
             for b in range(4):
                 unit("e1q", "e1p", "f1", b)
-        dma("s", T.kl[8 * r:8 * r + 8, :], (T[kf][0:128:16, :], v(kf)[1]))
-        scan(v("kr"), v("mw"), v(kf), 0.0, ALU.add, ALU.max)
-        ts(v("ko"), v("kr", 15, C, 16), v("corr"), None, ALU.subtract)
-        if r == 0:
-            zeros(v("zz", 128, 512))
-            zeros(v("gt", 128, 512))
-            zeros(v("mm1"))
         else:
             quant("vq", "vp", 0, 128, v("vs"))
+        mm(4, "skq", "skp", 0, "bq", "bp", 0, C)
+        act(v(kf), pb(4, 0, C), AF.Identity, bias=15.5)
+        dma("s", T.kl[8 * r:8 * r + 8, :], (T[kf][0:128:16, :],) + v(kf)[1:], after=[v(lp, 0, 96)])
+        scan(v("kr"), v("mw"), v(kf), 0.0, ALU.add, ALU.max)
+        ts(v("ko"), v("kr", 15, C, 16), v("corr"), None, ALU.subtract)
 
-        for b in range(4):
-            mm(4 + b, "e1q", "e1p", 128 * b, lq, lp, 0, 128)
-        for b in range(4):
-            act(v("ya", 64 * b, 64 * b + 64), pb(4 + b, 64, 128), AF.Copy)
-            tt(v("y2", b, 256, 4), pb(4 + b, 0, 64), v("ya", 64 * b, 64 * b + 64), ALU.max)
-        tt(v("zz", 0, 128), v("y2", 0, 128), v("y2", 128, 256), ALU.max)
-        quant("zq", "zp", 0, 128, v("zz"))
+        for k, b in enumerate((0, 2, 1, 3)):
+            mm(4 + k, "e1q", "e1p", 128 * b, lq, lp, 0, 128)
+            act(v("ya", 64 * b, 64 * b + 64), pb(4 + k, 64, 128), AF.Copy)
+            tt(v("y2", b, 256, 4), pb(4 + k, 0, 64), v("ya", 64 * b, 64 * b + 64), ALU.max)
+            if k % 2:
+                tt(v("at", k // 2, 128, 2), v("y2", k // 2, 128, 2), v("y2", 128 + k // 2, 256, 2), ALU.max)
+        quant("zq", "zp", 0, 128, v("at"))
         for b in range(4):
             mm(4 + b, "wq", "wp", 128 * b, "zq", "zp", 0, 128)
-        for b in range(4):
             if b % 2 == 0:
-                act(v("gt", b, 128, 4), pb(4 + b, 0, M), AF.Relu, scale=0.015625)
+                act(v("at", b, 128, 4), pb(4 + b, 0, M), AF.Relu, scale=0.015625)
             else:
-                ts(v("gt", b, 128, 4), pb(4 + b, 0, M), 0.0, 0.015625, ALU.max, ALU.mult)
-        quant("gq", "gp", 0, 128, v("gt"))
-        order = (0, 2, 1, 3)
-        for k, b in enumerate(order):
+                ts(v("at", b, 128, 4), pb(4 + b, 0, M), 0.0, 0.015625, ALU.max, ALU.mult)
+        quant("gq", "gp", 0, 128, v("at"))
+        for k, b in enumerate((2, 0, 3, 1)):
             mm(4 + k, "ehq", "ehp", 128 * b, "gq", "gp", 0, 128)
-
-        new = "st%d" % (r + 1)
-        go = first_products(r + 1)
-
-        def part(b, half):
-            a, e = RUNS[half]
-            return (v(new, 4 * a + b, 4 * e, 4), ind(v("gw", M * b, M * b + M), v("ko", a // 16, e // 16)),
-                    v("dh", C * b + a, C * b + e), pb(b, a, e))
-
-        for k, b in enumerate(order):
-            if k == 0:
+            if b < 2:
                 cp(v("gw", M * b, M * b + M), pb(4 + k, 0, M))
             else:
                 act(v("gw", M * b, M * b + M), pb(4 + k, 0, M), AF.Copy)
-        tmp = {}
-        for b in (2, 3):
-            tmp[b] = v("tm", CUT * (b - 2), CUT * (b - 1))
-            act(tmp[b], part(b, 0)[1], AF.Copy)
-        for b in (0, 1):
-            o, gath, d, _ = part(b, 0)
-            tt(o, gath, d, ALU.add)
-        for b in tmp:
-            o, _, _, dp = part(b, 0)
-            tt(o, tmp[b], dp, ALU.add)
-        go(0)
-        n = C - CUT
-        for b in range(4):
-            late = v("tm", 2 * CUT + n * b, 2 * CUT + n * b + n)
-            o, gath, _, dp = part(b, 1)
-            act(late, gath, AF.Copy)
-            tt(o, late, dp, ALU.add)
-        go(1)
+
+        new = "st%d" % (r + 1)
+
+        def gath(b, a, e):
+            return ind(v("gw", M * b, M * b + M), v("ko", a // 16, e // 16))
+
+        for b, a, e in PIECES:
+            act(v("tm", C * b + a, C * b + e), gath(b, a, e), AF.Copy)
+        for k, (ra, rb) in enumerate(pieces(CUTS[r + 1])):
+            for b, a, e in FUSED:
+                if a == ra:
+                    tt(v(new, 4 * a + b, 4 * e, 4), gath(b, a, e), v("dh", C * b + a, C * b + e), ALU.add)
+            for b, a, e in PIECES:
+                if a == ra:
+                    tt(v(new, 4 * a + b, 4 * e, 4), v("tm", C * b + a, C * b + e), pb(b, a, e), ALU.add)
+            first_products(r + 1, k)
 
     last = "xp%d" % ROUNDS
-    act(v("yf", 0, CUT), pb(4, 0, CUT), AF.Copy)
-    cp(v("yf", CUT, C), pb(5, 0, C - CUT))
-    dma("a", T.y[:, 0:CUT], v("yf", 0, CUT))
-    dma("s", T.y[:, CUT:C], v("yf", CUT, C))
     for k in range(4):
-        dma("a", T.osc[4 * k:4 * k + 4, :], (T[last][32 * k:32 * k + 4, :], v(last)[1]))
+        dma("aaas"[k], T.osc[4 * k:4 * k + 4, :], (T[last][32 * k:32 * k + 4, :],) + v(last)[1:])
 
-    count = {"v": 0, "a": 0, "t": 0, "g": 0}
-    known = {q: {} for q in eng}
-    n_dma, sent = 0, 0
     log = {}
     for i, op in enumerate(ops):
         q = op["q"]
@@ -441,11 +394,21 @@ def rank_program(g, core, T, topo):
             log.setdefault(name, []).append((i, q, cols, False))
         for name, cols in op["w"]:
             log.setdefault(name, []).append((i, q, cols, True))
+        op["need"] = need
+    place = {i: n for n, i in enumerate(ORDER)}
+    assert len(place) == len(ops) and all(place[j] < place[i] for i, op in enumerate(ops) for j in op["need"])
+
+    count = {"v": 0, "a": 0, "t": 0, "g": 0}
+    known = {q: {} for q in eng}
+    n_dma, sent = 0, 0
+    for i in ORDER:
+        op = ops[i]
+        q = op["q"]
         if op["kind"] == "x":
             op["tok"], op["clock"] = (op["sem"], op["n"]), {op["sem"]: op["n"]}
             continue
         mine = known[q]
-        for j in sorted(need, reverse=True):
+        for j in sorted(op["need"], key=lambda j: -place[j]):
             sem, n = ops[j]["tok"]
             if mine.get(sem, 0) < n:
                 eng[q].wait_ge(T.sem[sem], n)
@@ -470,3 +433,23 @@ def rank_program(g, core, T, topo):
         g.wait_ge(T.sem["q" + q], count[q])
     for k in range(n_dma):
         g.wait_ge(T.sem["d%d" % k], 16)
+
+
+ORDER = [
+    7, 32, 33, 8, 9, 10, 11, 28, 0, 1, 14, 24, 168, 2, 34, 12, 16, 15, 13, 3, 43, 23, 50, 73, 30, 38, 61, 47, 39, 65,
+    48, 31, 35, 63, 74, 22, 21, 17, 44, 20, 18, 19, 27, 25, 75, 29, 84, 5, 6, 4, 26, 76, 77, 94, 51, 85, 40, 45, 36,
+    81, 72, 86, 42, 82, 87, 95, 78, 52, 69, 83, 62, 64, 67, 49, 66, 68, 60, 96, 91, 79, 97, 92, 101, 88, 70, 71, 93,
+    80, 46, 59, 102, 98, 108, 104, 106, 110, 89, 130, 103, 99, 53, 131, 163, 116, 41, 90, 132, 100, 124, 133, 126,
+    125, 117, 118, 127, 54, 128, 129, 135, 134, 114, 166, 55, 165, 112, 56, 109, 107, 119, 137, 136, 120, 138, 121,
+    57, 122, 37, 58, 139, 140, 123, 115, 113, 105, 111, 144, 141, 142, 143, 149, 147, 145, 146, 150, 148, 151, 155,
+    153, 157, 152, 156, 158, 154, 164, 167, 171, 159, 169, 160, 170, 176, 175, 161, 174, 172, 177, 173, 162, 179,
+    305, 180, 184, 178, 191, 185, 181, 192, 188, 186, 182,
+    193, 189, 183, 190, 187, 194, 195, 198, 200, 199, 196, 201, 202, 197, 203, 204, 207, 211, 208, 209, 212, 205,
+    218, 210, 206, 214, 219, 213, 221, 216, 220, 217, 232, 215, 222, 234, 223, 235, 224, 233, 236, 225, 237, 226,
+    238, 229, 227, 239, 230, 240, 228, 243, 266, 241, 252, 231, 244, 267, 306, 250, 242, 272, 256, 258, 245, 254,
+    273, 259, 248, 268, 274, 307, 269, 246, 260, 275, 276, 249, 277, 271, 270, 247, 261, 279, 278, 262, 280, 255,
+    257, 281, 263, 282, 264, 265, 251, 253, 283, 285, 284, 286, 288, 291, 287, 289, 292, 295, 290, 293, 297, 296,
+    299, 298, 294, 300, 301, 309, 302, 310, 303, 304, 318, 308, 311, 319, 314, 312, 321, 320, 315, 313, 322, 316,
+    323, 317, 324, 325, 326, 332, 327, 330, 333, 328, 331, 329, 334, 337, 341, 338, 339, 342, 335, 348, 340, 336,
+    344, 349, 343, 351, 345, 350, 347, 358, 352, 346, 354, 353, 357, 355, 356, 359, 360, 361, 362, 363, 366, 364,
+    368, 365, 367, 369]

from concourse.bass import DstId, RemoteDMATransfer
from concourse.mybir import dt, AluOpType, ActivationFunctionType

ALU = AluOpType
AF = ActivationFunctionType
C, HC, M, ROUNDS = 448, 224, 32, 2
F16 = "float16"
OW = 496
TBW = 464
BF, F32, I32, U16, CODE, PLANE = "bfloat16", "float32", "int32", "uint16", "float8_e4m3fn_x4", "uint8"

CUTS = ((128, 320), (256,), (256,))
COUNT_CUTS = ((320,), (256,))
FUSED = ((0, 0, 256), (1, 0, 256), (0, 256, 448))
PIECES = ((2, 0, 256), (3, 0, 256), (1, 256, 448), (2, 256, 448), (3, 256, 448))
SORT_VECTOR = ((0, 0, 448), (3, 256, 448))
SORT_SCALAR = ((1, 0, 448), (2, 0, 448), (3, 0, 256))

WIDTHS = {
    BF: dict(st0=4 * C, st1=4 * C, st2=4 * C, us=512, vs=512, ones=512, hf=516, f1=516, fh=516, bt=4 * C, stt=1024,
             stk=512, tf=256, tk=128, mk=16, mw=C, hr=34, tb=2 * TBW, jv=512, sw=704, dh=4 * C, gs=4 * C,
             oo=4 * OW + 16, mm0=OW, mm1=OW, nb=32, at=512, ya=256, y2=256, gw=128, tm=4 * C),
    F32: dict(sg=4, dmf=16, m16a=16, m16b=16, cst=2, dc=2, ndm=1, corr=1, odd=1, dum=2, cc=6, junk=18, rw=3, hd=1,
              zj=2, zi=2, ci=32, bx=32, se=3, ed=2, kf0=C, kf1=C, yf=C),
    I32: dict(pi=4, ti=4, dmi=16, dmj=16),
    F16: dict(ta=2 * C, zs=2 * C, zt=2 * C, rb=2 * C, cb=HC, ct=HC, rr=32, wt=32, wr=C, kr=C),
    U16: dict(wo=32, lo=28, so=4, ko=28),
    CODE: dict(xq0=C, xq1=C, xq2=C, uq=128, vq=128, wq=512, ehq=512, e1q=512, bq=C, stq=256, skq=128,
               lq0=224, lq1=224, zq=128, gq=128),
    PLANE: dict(xp0=C, xp1=C, xp2=C, up=128, vp=128, wp=512, ehp=512, e1p=512, bp=C, stp=256, skp=128,
                lp0=224, lp1=224, zp=128, gp=128),
}
SCRATCH = {}
for _dtype, _bufs in WIDTHS.items():
    for _name, _w in _bufs.items():
        SCRATCH[_name] = ("sbuf", [128, _w], _dtype)
for _k in range(8):
    SCRATCH["pb%d" % _k] = ("psum", [128, 512], F32)
NDMA = 17
SEMAPHORES = ["qv", "qa", "qt", "qg", "sent", "arr0", "arr1"] + ["d%d" % _k for _k in range(NDMA)]


def rank_program(g, core, T, topo):
    rank = T.rank_of(core)
    if rank is None:
        return
    cores = [int(c) for c in T.cores]
    n_ranks = len(cores)
    ops = []
    eng = {"v": g.vector, "a": g.scalar, "t": g.tensor, "g": g, "s": g.sync}

    def v(name, a=0, b=None, s=1):
        if b is None:
            b = SCRATCH[name][1][1]
        ap = T[name][:, a:b] if s == 1 else T[name][:, a:b:s]
        cols = frozenset([0]) if name.startswith("pb") else frozenset(range(a, b, s))
        return (ap, [(name, cols)], len(range(a, b, s)))

    def ind(win, off):
        return (win[0].indirect(off[0]), win[1] + off[1], 16 * off[2])

    def ap(x):
        return x[0] if isinstance(x, tuple) else x

    def foot(xs):
        return [f for x in xs if isinstance(x, tuple) for f in x[1]]

    def add(q, kind, fn, reads, writes):
        ops.append(dict(q=q, kind=kind, fn=fn, r=foot(reads), w=foot(writes)))

    def ts(out, in0, s1, s2, op0, op1=None):
        if op1 is None:
            add("v", "c", lambda: g.vector.tensor_scalar(ap(out), ap(in0), ap(s1), None, op0), [in0, s1], [out])
        else:
            add("v", "c", lambda: g.vector.tensor_scalar(ap(out), ap(in0), ap(s1), ap(s2), op0, op1),
                [in0, s1, s2], [out])

    def tt(out, in0, in1, op):
        add("v", "c", lambda: g.vector.tensor_tensor(ap(out), ap(in0), ap(in1), op), [in0, in1], [out])

    def cp(out, in_):
        add("v", "c", lambda: g.vector.tensor_copy(ap(out), ap(in_)), [in_], [out])

    def scatter(win, off, in_):
        add("v", "c", lambda: g.vector.tensor_copy(win[0].indirect(off[0]), ap(in_)), [in_, off], [win])

    def mset(out, val):
        add("v", "c", lambda: g.vector.memset(ap(out), val), [], [out])

    def scan(out, d0, d1, init, op0, op1):
        add("v", "c", lambda: g.vector.tensor_tensor_scan(ap(out), ap(d0), ap(d1), ap(init), op0, op1),
            [d0, d1, init], [out])

    def tr(out, in_):
        add("v", "c", lambda: g.vector.transpose(ap(out), ap(in_)), [in_], [out])

    def quant(q, p, a, b, tile):
        add("v", "c", lambda: g.vector.quantize_mx(T[q][:, a:b], T[p][:, a:b], ap(tile)), [tile],
            [v(q, a, b), v(p, a, b)])

    def act(out, in_, func, bias=None, scale=None, accum=None):
        kw = {}
        if bias is not None:
            kw["bias"] = ap(bias)
        if scale is not None:
            kw["scale"] = ap(scale)
        if accum is not None:
            kw["accum_out"] = ap(accum)
        add("a", "c", lambda: g.scalar.activation(ap(out), ap(in_), func, **kw), [in_, bias, scale], [out, accum])

    def mm(bank, lq, lp, la, rq, rp, a, b):
        sides = [v(lq, la, la + 128), v(lp, la, la + 128), v(rq, a, b), v(rp, a, b)]
        out = v("pb%d" % bank, 0, b - a)
        add("t", "c", lambda: g.tensor.matmul_mx(out[0], sides[0][0], sides[1][0], sides[2][0], sides[3][0],
                                                 True, True), sides, [out])

    def pb(bank, a, b):
        return v("pb%d" % bank, a, b)

    def iota(out, pattern, base, cm, whole=False):
        if whole:
            add("g", "c", lambda: g.iota(ap(out), pattern, base, cm), [], [out])
        else:
            add("g", "c", lambda: g.iota(ap(out), pattern, base, cm, allow_small_or_imprecise_dtypes=True),
                [], [out])

    def zeros(out):
        iota(out, [[0, out[2]]], 0, 0)

    def sel(out, in_, pattern, op, fill, base, cm):
        add("g", "c", lambda: g.affine_select(ap(out), ap(in_), pattern, op, fill, base, cm), [in_], [out])

    def dma(q, out, in_, after=()):
        add(q, "d", lambda: eng[q].dma_start(ap(out), ap(in_)), [in_] + list(after), [out])

    def as_bytes(x):
        return (x[0].bitcast(dt.uint8),) + x[1:]

    def pieces(cuts):
        edges = (0,) + tuple(cuts) + (C,)
        return list(zip(edges, edges[1:]))

    dma("s", v("us"), T.u[:, :])
    for a, b in pieces(CUTS[0]):
        dma("s", v("st0", 4 * a, 4 * b), T.x[:, 4 * a:4 * b])
    dma("s", as_bytes(v("wq")), T.wc[:, :], after=[v("st0")])
    dma("s", v("wp"), T.ws[:, :], after=[v("st0")])
    dma("s", v("vs"), T.v[:, :], after=[v("st0")])

    mset(v("ones"), 1.0)
    for i in range(4):
        iota(v("pi", i, i + 1), [[0, 1]], 0, 8 >> i, True)
    ts(v("ti"), v("pi"), 3, 1, ALU.logical_shift_right, ALU.bitwise_and)
    ts(v("sg"), v("ti"), 2.0, -1.0, ALU.mult, ALU.add)
    sel(v("mk"), v("ones", 0, 16), [[0, 2], [-16, 8]], ALU.is_ge, 0.0, 0, 1)
    sel(v("mk"), v("mk"), [[0, 2], [16, 8]], ALU.is_ge, 0.0, 15, -1)
    mset(v("tf"), 0.0)
    for i in range(4):
        act(v("tf", i, 256, 16), v("mk"), AF.Copy, scale=v("sg", i, i + 1))
    for h in range(2):
        act(v("tf", 128 * h + 4, 128 * h + 128, 16), v("mk", 0, 8), AF.Copy, scale=2.0 * h - 1.0)
    mset(v("stt", 0, 512), 0.0)
    act(v("stt", 512, 1024), v("ones"), AF.Copy, scale=0.0)
    tr(v("stt", 0, 1024, 4), v("tf"))
    quant("stq", "stp", 0, 256, v("stt"))
    for a, b in pieces(CUTS[0])[:2]:
        mset(v("bt", 4 * a, 4 * b), 0.0)
    act(v("bt", 4 * C - 512, 4 * C), v("ones"), AF.Copy, scale=0.0)
    mset(v("hf"), 0.5)
    sel(v("fh"), v("hf"), [[1, 516]], ALU.is_equal, 0.0, -3, -4)
    iota(v("dmi"), [[1, 16]], 128, -1, True)
    ts(v("dmj"), v("dmi"), 15, None, ALU.bitwise_and)
    cp(v("dmf"), v("dmj"))
    iota(v("cst"), [[16, 2]], C + 16, 0)
    act(v("ndm"), v("dmf", 15, 16), AF.Copy, scale=-1.0)
    act(v("dc"), v("cst"), AF.Identity, bias=v("ndm"))
    zeros(v("tb", 0, 2 * TBW, TBW))
    iota(v("dum"), [[128, 2]], C - 511, 1)
    for hg in range(2):
        act(v("rr", 16 * hg + 14, 16 * hg + 16), v("dum"), AF.Copy)
    act(v("junk", 0, 4), v("mk", 1, 8, 2), AF.Identity, scale=float(C), bias=C / 4.0, accum=v("odd"))
    ts(v("zj"), v("dmf", 0, 16, 15), 0.0, -1024.0, ALU.is_equal, ALU.mult)
    act(v("hd"), v("zj", 0, 1), AF.Identity, bias=v("zj", 1, 2))
    act(v("zi", 0, 1), v("zj", 0, 1), AF.Identity, scale=-1.0, bias=1.0)
    act(v("zi", 1, 2), v("zj", 1, 2), AF.Copy)
    iota(v("hr"), [[0, 34]], 1024, 0)
    sel(v("hr", 1, 33), v("hr", 1, 33), [[0, 2], [1, 16]], ALU.is_gt, 0.0, -13, 0)
    iota(v("jv"), [[1, 32], [32, 16]], -HC, 0)
    ts(v("m16a"), v("dmf"), 0.0, -4096.0, ALU.is_equal, ALU.mult)
    ts(v("m16b"), v("dmf"), 1.0, 512.0, ALU.is_equal, ALU.mult)
    tt(v("mw", 0, 16), v("m16a"), v("m16b"), ALU.add)
    w = 16
    while w < C:
        n = min(w, C - w)
        act(v("mw", w, w + n), v("mw", 0, n), AF.Copy)
        w += n
    ts(v("corr"), v("dmf", 15, 16), 1.0, 512.0, ALU.min, ALU.mult)
    act(v("nb"), v("ones", 0, 32), AF.Copy, scale=-1e29)
    zeros(v("mm0"))
    zeros(v("oo", 0, 1))
    for b in range(4):
        zeros(v("oo", OW * b + C + 1, OW * (b + 1) + 1))
    zeros(v("at", 128, 512))
    zeros(v("tk"))
    zeros(v("stk"))

    def unit(q, p, src, b):
        quant(q, p, 128 * b, 128 * b + 128, v(src, 3 - b, 515 - b))

    for b in range(4):
        unit("ehq", "ehp", "fh", b)

    def first_products(r, k):
        rn = pieces(CUTS[r])
        a, b = rn[k]
        xq, xp, at = "xq%d" % r, "xp%d" % r, 4 + k % 2
        quant(xq, xp, a, b, v("st%d" % r, 4 * a, 4 * b))
        if r == ROUNDS:
            mm(at, "vq", "vp", 0, xq, xp, a, b)
            dma("s", T.oc[:, 4 * a:4 * b], as_bytes(v(xq, a, b)))
            if k == 0:
                act(v("yf", a, b), pb(at, 0, b - a), AF.Copy)
            else:
                cp(v("yf", a, b), pb(at, 0, b - a))
            dma("as"[k], T.y[:, a:b], v("yf", a, b))
            return
        mm(at, "uq", "up", 0, xq, xp, a, b)
        act(v("bt", 4 * a, 4 * b, 4), pb(at, 0, b - a), AF.Sign, bias=-1e-36)
        quant("bq", "bp", a, b, v("bt", 4 * a, 4 * b))
        final = k == len(rn) - 1
        for h in range(2):
            bank, n = (4 if final else 6) + h, 2 * k + h
            mm(bank, "stq", "stp", 128 * h, "bq", "bp", a, b)
            act(v("tb", TBW * h + 1 + a, TBW * h + 1 + b), pb(bank, 0, b - a), AF.Relu, bias=-2048.0,
                scale=512.0, accum=v("cc", n, n + 1))
            ts(v("ta", C * h + a, C * h + b), v("tb", TBW * h + 1 + a, TBW * h + 1 + b),
               (513.0 if h else 511.0) / 512, None, ALU.mult)

    quant("uq", "up", 0, 128, v("us"))
    for k in range(len(CUTS[0]) + 1):
        first_products(0, k)

    others = [k for k in range(n_ranks) if k != rank]
    mask = topo.mask(core, cores[others[0]])
    for k in others[1:]:
        mask &= topo.mask(core, cores[k])
    n_eng = bin(mask).count("1")

    for r in range(ROUNDS):
        xq, xp, lq, lp, mmr, kf = ["%s%d" % (s, r) for s in ("xq", "xp", "lq", "lp", "mm", "kf")]
        nk = len(CUTS[r]) + 1
        for b in range(4):
            mm(b, "ehq", "ehp", 128 * b, xq, xp, 0, C)
            act(v("dh", C * b, C * b + C), pb(b, 0, C), AF.Copy)
        for h in range(2):
            act(v("junk", 6 * h, 6 * h + nk), v("cc", h, 2 * nk, 2), AF.Copy, scale=1.0 / 512, accum=v("rw", h, h + 1))
            act(v("ed", h, h + 1), v("rw", h, h + 1), AF.Relu, bias=v("dc", h, h + 1), scale=-512.0)
        act(v("junk", 12, 12 + 2 * nk), v("cc", 0, 2 * nk), AF.Copy, scale=1.0 / 512, accum=v("rw", 2, 3))
        act(v("cb"), v("ones", 0, HC), AF.Identity, scale=v("hd"), bias=v("rw", 2, 3))
        tr(v("ct"), v("cb"))
        scan(v("ci"), v("ct", 0, 32), v("hr", 0, 32), 0.0, ALU.add, ALU.add)
        tr(v("bx"), v("ci"))
        act(v("se", 0, 1), v("bx", 0, 1), AF.Identity, scale=-1.0, bias=v("odd"))
        for c in range(2):
            act(v("se", c + 1, c + 2), v("rw", 1 - c, 2 - c), AF.Identity, bias=v("se", c, c + 1))
        for h in range(2):
            for a, e in pieces(COUNT_CUTS[r]):
                scan(v("zs", C * h + a, C * h + e), v("ta", C * h + a, C * h + e), v("tb", TBW * h + a, TBW * h + e),
                     v("zs", C * h + a - 1, C * h + a) if a else v("zi", h, h + 1), ALU.add, ALU.subtract)
                tr(v("zt", C * h + a, C * h + e), v("zs", C * h + a, C * h + e))
            for a in (0, HC):
                if h:
                    scan(v("rb", C + a, C + a + HC), v("ct"), v("zt", C + a, C + a + HC), 0.0, ALU.add, ALU.max)
                else:
                    scan(v("rb", a, a + HC), v("zt", a, a + HC), v("ct"), -2048.0, ALU.max, ALU.add)
        for hg in range(2):
            tt(v("rr", 16 * hg, 16 * hg + 14), v("rb", 16 * hg + 15, C, 32), v("rb", C + 16 * hg + 15, 2 * C, 32),
               ALU.max)
        tr(v("wt"), v("rr"))
        ts(v("wo"), v("wt"), 511.0, None, ALU.add)
        scatter(v("sw"), v("wo"), v("jv"))
        scan(v("wr"), v("mw"), v("sw", 0, C), 0.0, ALU.add, ALU.max)
        ts(v("lo"), v("wr", 15, C, 16), v("corr"), float(HC), ALU.subtract, ALU.add)
        for c in range(2):
            ts(v("so", c, 4, 2), v("se", 1 - c, 3 - c), v("ed", c, c + 1), None, ALU.max)
        scatter(v(mmr), v("so", 0, 2), v("nb"))

        def sorted_part(b, a, e):
            return v("gs", C * b + a, C * b + e), ind(v("dh", C * b, C * b + C), v("lo", a // 16, e // 16))

        def ends(b):
            return v("at", b, 128, 4), ind(v("oo", OW * b, OW * b + C + 33), v("so", 2, 4))

        for piece in SORT_SCALAR:
            act(*sorted_part(*piece), AF.Copy)
        for piece in SORT_VECTOR:
            cp(*sorted_part(*piece))
        for b in range(4):
            scan(v("oo", OW * b + 1, OW * b + 1 + C), v(mmr, 0, C), v("gs", C * b, C * b + C), 0.0, ALU.add, ALU.max)
            if b < 3:
                act(*ends(b), AF.Copy, scale=2.0)
        ts(*ends(3), 2.0, None, ALU.mult)
        quant(lq, lp, 96, 224, v("at"))

        def send(buf, code, r=r):
            src = v(buf, 96, 128)
            ids, dsts = [], []
            for k in others:
                slot = [j for j in range(n_ranks) if j != k].index(rank)
                d = v(buf, M * slot, M * slot + M)
                rid, pid, _ = topo.addr(cores[k])
                ids.append(DstId(rid=int(rid), pnc=int(pid)))
                dsts.append(as_bytes(d)[0] if code else d[0])
            s = as_bytes(src)[0] if code else src[0]
            add("g", "r", lambda: g.remote_dma_fused(
                [RemoteDMATransfer(dst_ids=ids, dma_engine_mask=mask, remote_sem=T.sem["arr%d" % r],
                                   srcs=[s], dsts=dsts)], local_sem=T.sem.sent), [src], [])
        send(lq, True)
        send(lp, False)
        ops.append(dict(q="x", kind="x", sem="arr%d" % r, n=2 * n_eng * len(others), r=[],
                        w=foot([v(lq, 0, 96), v(lp, 0, 96)])))

        if r == 0:
            for i in range(5):
                act(v("tk", i, 128, 16), v("mk", 0, 8), AF.Copy, scale=2.0 ** (i - 1))
            act(v("mm1"), v("ones", 0, OW), AF.Copy, scale=0.0)
            tr(v("stk", 0, 512, 4), v("tk"))
            quant("skq", "skp", 0, 128, v("stk"))
            act(v("f1"), v("fh"), AF.Copy, scale=2.0)
            for b in range(4):
                unit("e1q", "e1p", "f1", b)
        else:
            quant("vq", "vp", 0, 128, v("vs"))
        mm(4, "skq", "skp", 0, "bq", "bp", 0, C)
        act(v(kf), pb(4, 0, C), AF.Identity, bias=15.5)
        dma("s", T.kl[8 * r:8 * r + 8, :], (T[kf][0:128:16, :],) + v(kf)[1:], after=[v(lp, 0, 96)])
        scan(v("kr"), v("mw"), v(kf), 0.0, ALU.add, ALU.max)
        ts(v("ko"), v("kr", 15, C, 16), v("corr"), None, ALU.subtract)

        for k, b in enumerate((0, 2, 1, 3)):
            mm(4 + k, "e1q", "e1p", 128 * b, lq, lp, 0, 128)
            act(v("ya", 64 * b, 64 * b + 64), pb(4 + k, 64, 128), AF.Copy)
            tt(v("y2", b, 256, 4), pb(4 + k, 0, 64), v("ya", 64 * b, 64 * b + 64), ALU.max)
            if k % 2:
                tt(v("at", k // 2, 128, 2), v("y2", k // 2, 128, 2), v("y2", 128 + k // 2, 256, 2), ALU.max)
        quant("zq", "zp", 0, 128, v("at"))
        for b in range(4):
            mm(4 + b, "wq", "wp", 128 * b, "zq", "zp", 0, 128)
            if b % 2 == 0:
                act(v("at", b, 128, 4), pb(4 + b, 0, M), AF.Relu, scale=0.015625)
            else:
                ts(v("at", b, 128, 4), pb(4 + b, 0, M), 0.0, 0.015625, ALU.max, ALU.mult)
        quant("gq", "gp", 0, 128, v("at"))
        for k, b in enumerate((2, 0, 3, 1)):
            mm(4 + k, "ehq", "ehp", 128 * b, "gq", "gp", 0, 128)
            if b < 2:
                cp(v("gw", M * b, M * b + M), pb(4 + k, 0, M))
            else:
                act(v("gw", M * b, M * b + M), pb(4 + k, 0, M), AF.Copy)

        new = "st%d" % (r + 1)

        def gath(b, a, e):
            return ind(v("gw", M * b, M * b + M), v("ko", a // 16, e // 16))

        for b, a, e in PIECES:
            act(v("tm", C * b + a, C * b + e), gath(b, a, e), AF.Copy)
        for k, (ra, rb) in enumerate(pieces(CUTS[r + 1])):
            for b, a, e in FUSED:
                if a == ra:
                    tt(v(new, 4 * a + b, 4 * e, 4), gath(b, a, e), v("dh", C * b + a, C * b + e), ALU.add)
            for b, a, e in PIECES:
                if a == ra:
                    tt(v(new, 4 * a + b, 4 * e, 4), v("tm", C * b + a, C * b + e), pb(b, a, e), ALU.add)
            first_products(r + 1, k)

    last = "xp%d" % ROUNDS
    for k in range(4):
        dma("aaas"[k], T.osc[4 * k:4 * k + 4, :], (T[last][32 * k:32 * k + 4, :],) + v(last)[1:])

    log = {}
    for i, op in enumerate(ops):
        q = op["q"]
        need = set()
        for name, cols in op["r"]:
            for j, jq, jc, jw in log.get(name, []):
                if (jw or (name.startswith("pb") and jq != q)) and not cols.isdisjoint(jc):
                    need.add(j)
        for name, cols in op["w"]:
            for j, jq, jc, jw in log.get(name, []):
                if not cols.isdisjoint(jc):
                    need.add(j)
        for name, cols in op["r"]:
            log.setdefault(name, []).append((i, q, cols, False))
        for name, cols in op["w"]:
            log.setdefault(name, []).append((i, q, cols, True))
        op["need"] = need
    place = {i: n for n, i in enumerate(ORDER)}
    assert len(place) == len(ops) and all(place[j] < place[i] for i, op in enumerate(ops) for j in op["need"])

    count = {"v": 0, "a": 0, "t": 0, "g": 0}
    known = {q: {} for q in eng}
    n_dma, sent = 0, 0
    for i in ORDER:
        op = ops[i]
        q = op["q"]
        if op["kind"] == "x":
            op["tok"], op["clock"] = (op["sem"], op["n"]), {op["sem"]: op["n"]}
            continue
        mine = known[q]
        for j in sorted(op["need"], key=lambda j: -place[j]):
            sem, n = ops[j]["tok"]
            if mine.get(sem, 0) < n:
                eng[q].wait_ge(T.sem[sem], n)
                for s2, n2 in ops[j]["clock"].items():
                    mine[s2] = max(mine.get(s2, 0), n2)
        ins = op["fn"]()
        if op["kind"] == "c":
            count[q] += 1
            op["tok"] = ("q" + q, count[q])
            ins.then_inc(T.sem["q" + q], 1)
        elif op["kind"] == "d":
            op["tok"] = ("d%d" % n_dma, 16)
            ins.then_inc(T.sem["d%d" % n_dma], 16)
            n_dma += 1
        else:
            sent += n_eng
            op["tok"] = ("sent", sent)
        op["clock"] = dict(mine)
        op["clock"][op["tok"][0]] = op["tok"][1]
    g.wait_ge(T.sem.sent, sent)
    for q in count:
        g.wait_ge(T.sem["q" + q], count[q])
    for k in range(n_dma):
        g.wait_ge(T.sem["d%d" % k], 16)


ORDER = [
    7, 32, 33, 8, 9, 10, 11, 28, 0, 1, 14, 24, 168, 2, 34, 12, 16, 15, 13, 3, 43, 23, 50, 73, 30, 38, 61, 47, 39, 65,
    48, 31, 35, 63, 74, 22, 21, 17, 44, 20, 18, 19, 27, 25, 75, 29, 84, 5, 6, 4, 26, 76, 77, 94, 51, 85, 40, 45, 36,
    81, 72, 86, 42, 82, 87, 95, 78, 52, 69, 83, 62, 64, 67, 49, 66, 68, 60, 96, 91, 79, 97, 92, 101, 88, 70, 71, 93,
    80, 46, 59, 102, 98, 108, 104, 106, 110, 89, 130, 103, 99, 53, 131, 163, 116, 41, 90, 132, 100, 124, 133, 126,
    125, 117, 118, 127, 54, 128, 129, 135, 134, 114, 166, 55, 165, 112, 56, 109, 107, 119, 137, 136, 120, 138, 121,
    57, 122, 37, 58, 139, 140, 123, 115, 113, 105, 111, 144, 141, 142, 143, 149, 147, 145, 146, 150, 148, 151, 155,
    153, 157, 152, 156, 158, 154, 164, 167, 171, 159, 169, 160, 170, 176, 175, 161, 174, 172, 177, 173, 162, 179,
    305, 180, 184, 178, 191, 185, 181, 192, 188, 186, 182,
    193, 189, 183, 190, 187, 194, 195, 198, 200, 199, 196, 201, 202, 197, 203, 204, 207, 211, 208, 209, 212, 205,
    218, 210, 206, 214, 219, 213, 221, 216, 220, 217, 232, 215, 222, 234, 223, 235, 224, 233, 236, 225, 237, 226,
    238, 229, 227, 239, 230, 240, 228, 243, 266, 241, 252, 231, 244, 267, 306, 250, 242, 272, 256, 258, 245, 254,
    273, 259, 248, 268, 274, 307, 269, 246, 260, 275, 276, 249, 277, 271, 270, 247, 261, 279, 278, 262, 280, 255,
    257, 281, 263, 282, 264, 265, 251, 253, 283, 285, 284, 286, 288, 291, 287, 289, 292, 295, 290, 293, 297, 296,
    299, 298, 294, 300, 301, 309, 302, 310, 303, 304, 318, 308, 311, 319, 314, 312, 321, 320, 315, 313, 322, 316,
    323, 317, 324, 325, 326, 332, 327, 330, 333, 328, 331, 329, 334, 337, 341, 338, 339, 342, 335, 348, 340, 336,
    344, 349, 343, 351, 345, 350, 347, 358, 352, 346, 354, 353, 357, 355, 356, 359, 360, 361, 362, 363, 366, 364,
    368, 365, 367, 369]
